import numpy as np
import ml_dtypes


def mxq(x, axis, fmt="e4m3"):
    dtype, down = {"e4m3": (ml_dtypes.float8_e4m3fn, 7), "e5m2": (ml_dtypes.float8_e5m2, 14)}[fmt]
    v = np.moveaxis(np.asarray(x, np.float32).astype(ml_dtypes.bfloat16).astype(np.float64), axis, -1)
    blocks = v.reshape(v.shape[:-1] + (-1, 32))
    amax = np.abs(blocks).max(-1, keepdims=True)
    byte = np.maximum(np.where(amax > 0, np.frexp(amax)[1] - 1 + 127, 0) - down, 1)
    scale = np.exp2(byte - 127.0)
    codes = (blocks / scale).astype(np.float32).astype(dtype).astype(np.float64)
    return np.moveaxis((codes * scale).reshape(v.shape), -1, axis)


WIDE = False


def mx_kscale(k):
    if not WIDE:
        return np.ones(k)
    levels = np.array([10, -10, 5, -5, 0])
    if k % 512:
        return np.exp2(np.random.permutation(np.resize(levels, k // 32))).repeat(32)
    a = np.empty((k // 512, 16))
    for p in range(k // 512):
        a[p, :8] = np.random.permutation(np.resize(levels, 8))
        for g in range(8):
            far = levels[np.abs(levels - a[p, g]) >= 10]
            a[p, g + 8] = far[np.random.randint(len(far))]
    return np.exp2(a.ravel()).repeat(32)


def f64(x):
    return np.asarray(x).astype(np.float64)


def striped(idx):
    return np.tile(idx.reshape(-1, 16).T, (8, 1)).astype(np.uint16)


def unstriped(offs):
    return offs[:16].T.reshape(-1).astype(np.int64)


E2M1 = np.array([0.0, 0.5, 1.0, 1.5, 2.0, 3.0, 4.0, 6.0, -0.0, -0.5, -1.0, -1.5, -2.0, -3.0, -4.0, -6.0])


def pack_weight(w, fmt):
    k, n = w.shape
    w = f64(np.asarray(w, np.float32).astype(ml_dtypes.bfloat16)).reshape(k // 32, 32, n)
    amax = np.abs(w).max(1)
    if fmt == "e4m3":
        byte = np.frexp(amax)[1] - 1 + 127 - 7
    else:
        mant, ex = np.frexp(amax / 6.0)
        byte = np.where(mant > 0.5, ex, ex - 1) + 127
    byte = np.clip(np.where(amax > 0, byte, 1), 1, 254)
    scaled = (w * np.exp2(127.0 - byte)[:, None, :]).reshape(k, n).astype(np.float32)
    by_word = np.ascontiguousarray(scaled.reshape(k // 512, 128, 4, n).transpose(0, 1, 3, 2))
    if fmt == "e4m3":
        words = by_word.astype(ml_dtypes.float8_e4m3fn).view(np.uint8)
    else:
        c = by_word.astype(ml_dtypes.float4_e2m1fn).view(np.uint8) & 0xF
        words = (c[..., 0::2] | (c[..., 1::2] << 4)).reshape(k // 512, 128, 2 * n)
    return np.ascontiguousarray(words), np.ascontiguousarray(byte.astype(np.uint8).reshape(k // 512, 16, n))


def unpack_weight(words, scales, fmt):
    g, _, n = scales.shape
    words = np.ascontiguousarray(words).reshape(g, 128, n, -1)
    if fmt == "e4m3":
        vals = words.view(ml_dtypes.float8_e4m3fn).astype(np.float64)
    else:
        nib = np.empty((g, 128, n, 4), np.uint8)
        nib[..., 0::2] = words & 0xF
        nib[..., 1::2] = words >> 4
        vals = E2M1[nib]
    vals = vals * np.repeat(np.exp2(scales.astype(np.float64) - 127.0), 8, axis=1)[..., None]
    return vals.transpose(0, 1, 3, 2).reshape(g * 512, n)


K, T, E1, C1, E2, C2, H = 256, 512, 2, 256, 2, 256, 512
N = 512


def by_expert(wq, xq, E, C):
    return np.concatenate([wq[e].T @ xq[:, e * C:(e + 1) * C] for e in range(E)], axis=1)


def setup_inputs():
    n = np.random.standard_normal
    v = mx_kscale(N)
    u = mx_kscale(H)
    slots1, slots2 = np.random.permutation(T), np.random.permutation(T)
    dy = pack_weight(n((N, T)) * v[:, None], "e4m3")
    w2t = pack_weight(n((N, H)) / np.sqrt(N) / v[:, None] * u, "e2m1")
    wat = [pack_weight(m, "e2m1") for m in n((E1, H, K)) / np.sqrt(H) / u[None, :, None]]
    wbt = [pack_weight(m, "e2m1") for m in n((E2, H, K)) / np.sqrt(H) / u[None, :, None]]
    return {
        "dy_words": dy[0],
        "dy_scales": dy[1],
        "w2t_words": w2t[0],
        "w2t_scales": w2t[1],
        "wat_words": np.stack([m[0] for m in wat]),
        "wat_scales": np.stack([m[1] for m in wat]),
        "wbt_words": np.stack([m[0] for m in wbt]),
        "wbt_scales": np.stack([m[1] for m in wbt]),
        "a": (n((H, T))).astype(np.float32),
        "c": (n((H, T))).astype(np.float32),
        "offs": striped(slots1),
        "offs2": striped(slots2),
    }


def reference(dy_words, dy_scales, w2t_words, w2t_scales, wat_words, wat_scales, wbt_words, wbt_scales, a, c, offs, offs2):
    w2t = unpack_weight(w2t_words, w2t_scales, "e2m1")
    wat = np.stack([unpack_weight(wat_words[e], wat_scales[e], "e2m1") for e in range(E1)])
    wbt = np.stack([unpack_weight(wbt_words[e], wbt_scales[e], "e2m1") for e in range(E2)])
    idx, idx2 = unstriped(offs), unstriped(offs2)
    dh = w2t.T @ unpack_weight(dy_words, dy_scales, "e4m3")
    da = dh * f64(c)
    dc = dh * f64(a)
    out = np.zeros((K, T))
    out[:, idx] = by_expert(wat, mxq(da[:, idx], 0, "e4m3"), E1, C1)
    out[:, idx2] += by_expert(wbt, mxq(dc[:, idx2], 0, "e4m3"), E2, C2)
    return out

@@ -1,0 +1,180 @@
+from contextlib import ExitStack
+
+import concourse.mybir as mybir
+
+K, T, H, N = 256, 512, 512, 512
+E, C = 2, 256
+FLOPS = 2 * N * H * T + 2 * 2 * H * K * T
+
+F32 = mybir.dt.float32
+BF16 = mybir.dt.bfloat16
+I32 = mybir.dt.int32
+U32 = mybir.dt.uint32
+U16 = mybir.dt.uint16
+U8 = mybir.dt.uint8
+FP8X4 = mybir.dt.float8_e4m3fn_x4
+FP4X4 = mybir.dt.float4_e2m1fn_x4
+MULT = mybir.AluOpType.mult
+ADD = mybir.AluOpType.add
+COPY = mybir.ActivationFunctionType.Copy
+P = 128
+HALF = 256
+LC = C // 16
+
+
+def tile_moe_plb_none_kernel(
+    tc, dy_words, dy_scales, w2t_words, w2t_scales, wat_words, wat_scales, wbt_words, wbt_scales, a, c, offs, offs2, out
+):
+    nc = tc.nc
+    with ExitStack() as ctx:
+        sb = ctx.enter_context(tc.tile_pool(name="sb", bufs=1))
+        ps = ctx.enter_context(tc.psum_pool(name="ps", bufs=1))
+
+        def tile(name, shape, dtype):
+            return sb.tile(shape, dtype, name=name, align_bytes=64)
+
+        list_a = tile("list_a", [P, T // 16], U16)
+        list_b = tile("list_b", [P, T // 16], U16)
+        w2_raw = tile("w2_raw", [P, 2 * H], U8)
+        first_sc = tile("first_sc", [P, H + T], U8)
+        w2_sc_raw = first_sc[:, 0:H]
+        dy_sc = first_sc[:, H:H + T]
+        w2 = tile("w2", [P, 2 * H], U8)
+        w2_sc = tile("w2_sc", [P, H], U8)
+        dy = tile("dy", [P, T], U32)
+        wa = tile("wa", [P, E, 2 * K], U8)
+        wb = tile("wb", [P, E, 2 * K], U8)
+        wa_sc = tile("wa_sc", [P, E, K], U8)
+        wb_sc = tile("wb_sc", [P, E, K], U8)
+        c_sb = tile("c_sb", [P, 4, T], F32)
+        a_sb = tile("a_sb", [P, 4, T], F32)
+
+        nc.gpsimd.memset(first_sc[:].bitcast(I32), 0)
+        for plane in (wa_sc, wb_sc):
+            nc.vector.memset(plane[:].rearrange("p e k -> p (e k)").bitcast(I32), 0)
+
+        def rows(q):
+            return slice(32 * q, 32 * q + 4), slice(4 * q, 4 * q + 4)
+
+        def load_scales(eng, dst, src, q):
+            part, row = rows(q)
+            eng.dma_start(out=dst[part, :].bitcast(I32), in_=src[0, row, :].bitcast(I32))
+
+        def load_expert(words, scales, w_src, s_src):
+            nc.sync.dma_start(out=words[:].bitcast(I32), in_=w_src[:, 0].rearrange("e p n -> p e n").bitcast(I32))
+            for q in range(4):
+                part, row = rows(q)
+                nc.sync.dma_start(out=scales[part].bitcast(I32), in_=s_src[:, 0, row, :].rearrange("e r n -> r e n").bitcast(I32))
+
+        c_v = c.rearrange("(p j) t -> p j t", j=4)
+        a_v = a.rearrange("(p j) t -> p j t", j=4)
+        for q in range(4):
+            load_scales(nc.sync, w2_sc_raw, w2t_scales, q)
+        nc.sync.dma_start(out=w2_raw[:].bitcast(I32), in_=w2t_words[0].bitcast(I32))
+        nc.sync.dma_start(out=dy[:].bitcast(I32), in_=dy_words[0].rearrange("p t d -> p (t d)").bitcast(I32))
+        for q in range(4):
+            load_scales(nc.sync, dy_sc, dy_scales, q)
+        for th in range(2):
+            nc.sync.dma_start(out=c_sb[:, 0:2, th * HALF:(th + 1) * HALF], in_=c_v[:, 0:2, th * HALF:(th + 1) * HALF])
+        nc.sync.dma_start(list_a[:], offs)
+        nc.sync.dma_start(out=c_sb[:, 2:4, :], in_=c_v[:, 2:4, :])
+        for h in range(2):
+            nc.sync.dma_start(out=a_sb[:, 2 * h:2 * h + 2, :], in_=a_v[:, 2 * h:2 * h + 2, :])
+        nc.sync.dma_start(list_b[:], offs2)
+        load_expert(wa, wa_sc, wat_words, wat_scales)
+        load_expert(wb, wb_sc, wbt_words, wbt_scales)
+
+        w2_in = w2_raw[:].bitcast(U16).rearrange("p (m j) -> p j m", j=4)
+        w2_out = w2[:].bitcast(U16).rearrange("p (j m) -> p j m", j=4)
+        sc_in = w2_sc_raw.rearrange("p (m j) -> p j m", j=4)
+        sc_out = w2_sc[:].rearrange("p (j m) -> p j m", j=4)
+
+        dh_ps = [[ps.tile([P, 2, HALF], F32, name=f"dh_ps{h}{th}") for th in range(2)] for h in range(2)]
+        for h in range(2):
+            nc.vector.tensor_copy(out=sc_out[:, 2 * h:2 * h + 2, :], in_=sc_in[:, 2 * h:2 * h + 2, :])
+            nc.vector.tensor_copy(out=w2_out[:, 2 * h:2 * h + 2, :], in_=w2_in[:, 2 * h:2 * h + 2, :])
+        for h in range(2):
+            for th in range(2):
+                for i in range(2):
+                    j = 2 * h + i
+                    nc.tensor.matmul_mx(
+                        out=dh_ps[h][th][:, i, :],
+                        lhsT=w2[:, 2 * P * j:2 * P * (j + 1)].bitcast(FP4X4),
+                        lhsT_scale=w2_sc[:, P * j:P * (j + 1)],
+                        rhs=dy[:, th * HALF:(th + 1) * HALF].bitcast(FP8X4),
+                        rhs_scale=dy_sc[:, th * HALF:(th + 1) * HALF],
+                        start=True, stop=True,
+                    )
+
+        da_pairs = [tile(f"da_pairs{h}", [P, T, 2], BF16) for h in range(2)]
+        da_got = [tile(f"da_got{e}", [P, 2, C], U32) for e in range(E)]
+        da_slots = [tile(f"da_slots{e}", [P, C, 4], BF16) for e in range(E)]
+        dc_slots = [tile(f"dc_slots{e}", [P, C, 4], BF16) for e in range(E)]
+        dc_planes = [tile(f"dc_planes{j}", [P, T], BF16) for j in range(4)]
+        dh_sb = tile("dh_sb", [P, 4, T], F32)
+
+        for h in range(2):
+            for th in range(2):
+                tok = slice(th * HALF, (th + 1) * HALF)
+                nc.vector.tensor_tensor(
+                    out=da_pairs[h][:, tok, :],
+                    in0=dh_ps[h][th][:].rearrange("p i t -> p t i"),
+                    in1=c_sb[:, 2 * h:2 * h + 2, tok].rearrange("p i t -> p t i"),
+                    op=MULT,
+                )
+            window = da_pairs[h][:].rearrange("p t i -> p (t i)").bitcast(U32)
+            for e in range(E):
+                nc.vector.tensor_copy(out=da_got[e][:, h, :], in_=window.indirect(list_a[:, e * LC:(e + 1) * LC]))
+
+        def products(name, slots, words, scales, e):
+            codes = tile(f"{name}_codes{e}", [P, C], U32)
+            codes_sc = tile(f"{name}_codes_sc{e}", [P, C], U8)
+            nc.vector.quantize_mx(out=codes[:].bitcast(FP8X4), scales=codes_sc[:], in_=slots[:].rearrange("p s j -> p (s j)"))
+            acc = ps.tile([P, 2, C], F32, name=f"{name}_ps{e}")
+            res = tile(f"{name}_sb{e}", [P, 2, C], F32)
+            for kh in range(2):
+                nc.tensor.matmul_mx(
+                    out=acc[:, kh, :],
+                    lhsT=words[:, e, 2 * P * kh:2 * P * (kh + 1)].bitcast(FP4X4),
+                    lhsT_scale=scales[:, e, P * kh:P * (kh + 1)],
+                    rhs=codes[:].bitcast(FP8X4),
+                    rhs_scale=codes_sc[:],
+                    start=True, stop=True,
+                )
+            for kh in range(2):
+                nc.scalar.activation(out=res[:, kh, :], in_=acc[:, kh, :], func=COPY)
+            return res
+
+        r_sb = []
+        for e in range(E):
+            nc.scalar.copy(
+                out=da_slots[e][:].rearrange("p s (h i) -> p s h i", h=2),
+                in_=da_got[e][:].bitcast(BF16).rearrange("p h (s i) -> p s h i", i=2),
+            )
+            r_sb.append(products("r", da_slots[e], wa, wa_sc, e))
+
+        for h in range(2):
+            for th in range(2):
+                nc.scalar.activation(out=dh_sb[:, 2 * h:2 * h + 2, th * HALF:(th + 1) * HALF], in_=dh_ps[h][th][:], func=COPY)
+        for j in range(4):
+            nc.gpsimd.tensor_tensor(out=dc_planes[j][:], in0=dh_sb[:, j, :], in1=a_sb[:, j, :], op=MULT)
+
+        q_sb = []
+        for e in range(E):
+            for j in range(4):
+                nc.scalar.activation(out=dc_slots[e][:, :, j], in_=dc_planes[j][:].indirect(list_b[:, e * LC:(e + 1) * LC]), func=COPY)
+            q_sb.append(products("q", dc_slots[e], wb, wb_sc, e))
+
+        r_tok = [tile(f"r_tok{kh}", [P, T], F32) for kh in range(2)]
+        q_tok = [tile(f"q_tok{kh}", [P, T], F32) for kh in range(2)]
+        total = [tile(f"total{kh}", [P, T], F32) for kh in range(2)]
+        for tok, res, lst in ((r_tok, r_sb, list_a), (q_tok, q_sb, list_b)):
+            for e in range(E):
+                for kh in range(2):
+                    nc.vector.tensor_copy(out=tok[kh][:].indirect(lst[:, e * LC:(e + 1) * LC]), in_=res[e][:, kh, :])
+        nc.gpsimd.tensor_tensor(out=total[0][:], in0=r_tok[0][:], in1=q_tok[0][:], op=ADD)
+        nc.sync.dma_start(out=out[0:P, :], in_=total[0][:])
+        for th in range(2):
+            tok = slice(th * HALF, (th + 1) * HALF)
+            nc.vector.tensor_tensor(out=total[1][:, tok], in0=r_tok[1][:, tok], in1=q_tok[1][:, tok], op=ADD)
+            (nc.scalar if th == 0 else nc.sync).dma_start(out=out[P:2 * P, tok], in_=total[1][:, tok])

@@ -30,18 +30,17 @@ def tile_moe_plb_none_kernel(
         sb = ctx.enter_context(tc.tile_pool(name="sb", bufs=1))
         ps = ctx.enter_context(tc.psum_pool(name="ps", bufs=1))
 
-        def tile(name, shape, dtype):
-            return sb.tile(shape, dtype, name=name, align_bytes=64)
+        def tile(name, shape, dtype, tag=None):
+            return sb.tile(shape, dtype, name=name, tag=tag or name, align_bytes=64)
 
         list_a = tile("list_a", [P, T // 16], U16)
         list_b = tile("list_b", [P, T // 16], U16)
         w2_raw = tile("w2_raw", [P, 2 * H], U8)
-        first_sc = tile("first_sc", [P, H + T], U8)
-        w2_sc_raw = first_sc[:, 0:H]
-        dy_sc = first_sc[:, H:H + T]
+        w2_sc_raw = tile("w2_sc_raw", [P, H], U8)
         w2 = tile("w2", [P, 2 * H], U8)
         w2_sc = tile("w2_sc", [P, H], U8)
         dy = tile("dy", [P, T], U32)
+        dy_sc = tile("dy_sc", [P, T], U8)
         wa = tile("wa", [P, E, 2 * K], U8)
         wb = tile("wb", [P, E, 2 * K], U8)
         wa_sc = tile("wa_sc", [P, E, K], U8)
@@ -49,9 +48,7 @@ def tile_moe_plb_none_kernel(
         c_sb = tile("c_sb", [P, 4, T], F32)
         a_sb = tile("a_sb", [P, 4, T], F32)
 
-        nc.gpsimd.memset(first_sc[:].bitcast(I32), 0)
-        for plane in (wa_sc, wb_sc):
-            nc.vector.memset(plane[:].rearrange("p e k -> p (e k)").bitcast(I32), 0)
+        nc.vector.memset(w2_sc_raw[:].bitcast(I32), 0)
 
         def rows(q):
             return slice(32 * q, 32 * q + 4), slice(4 * q, 4 * q + 4)
@@ -68,25 +65,27 @@ def tile_moe_plb_none_kernel(
 
         c_v = c.rearrange("(p j) t -> p j t", j=4)
         a_v = a.rearrange("(p j) t -> p j t", j=4)
-        for q in range(4):
-            load_scales(nc.sync, w2_sc_raw, w2t_scales, q)
+        for q in range(2):
+            load_scales(nc.sync, dy_sc, dy_scales, q)
         nc.sync.dma_start(out=w2_raw[:].bitcast(I32), in_=w2t_words[0].bitcast(I32))
         nc.sync.dma_start(out=dy[:].bitcast(I32), in_=dy_words[0].rearrange("p t d -> p (t d)").bitcast(I32))
         for q in range(4):
+            load_scales(nc.sync, w2_sc_raw, w2t_scales, q)
+        for q in range(2, 4):
             load_scales(nc.sync, dy_sc, dy_scales, q)
         for th in range(2):
             nc.sync.dma_start(out=c_sb[:, 0:2, th * HALF:(th + 1) * HALF], in_=c_v[:, 0:2, th * HALF:(th + 1) * HALF])
         nc.sync.dma_start(list_a[:], offs)
+        nc.sync.dma_start(out=a_sb[:, 0:2, :], in_=a_v[:, 0:2, :])
         nc.sync.dma_start(out=c_sb[:, 2:4, :], in_=c_v[:, 2:4, :])
-        for h in range(2):
-            nc.sync.dma_start(out=a_sb[:, 2 * h:2 * h + 2, :], in_=a_v[:, 2 * h:2 * h + 2, :])
         nc.sync.dma_start(list_b[:], offs2)
         load_expert(wa, wa_sc, wat_words, wat_scales)
+        nc.sync.dma_start(out=a_sb[:, 2:4, :], in_=a_v[:, 2:4, :])
         load_expert(wb, wb_sc, wbt_words, wbt_scales)
 
         w2_in = w2_raw[:].bitcast(U16).rearrange("p (m j) -> p j m", j=4)
         w2_out = w2[:].bitcast(U16).rearrange("p (j m) -> p j m", j=4)
-        sc_in = w2_sc_raw.rearrange("p (m j) -> p j m", j=4)
+        sc_in = w2_sc_raw[:].rearrange("p (m j) -> p j m", j=4)
         sc_out = w2_sc[:].rearrange("p (j m) -> p j m", j=4)
 
         dh_ps = [[ps.tile([P, 2, HALF], F32, name=f"dh_ps{h}{th}") for th in range(2)] for h in range(2)]
@@ -106,32 +105,40 @@ def tile_moe_plb_none_kernel(
                         start=True, stop=True,
                     )
 
-        da_pairs = [tile(f"da_pairs{h}", [P, T, 2], BF16) for h in range(2)]
-        da_got = [tile(f"da_got{e}", [P, 2, C], U32) for e in range(E)]
-        da_slots = [tile(f"da_slots{e}", [P, C, 4], BF16) for e in range(E)]
+        da_pairs = [tile(f"da_pairs{h}", [P, 2 * T], BF16) for h in range(2)]
+        da_slots = [tile(f"da_slots{e}", [P, 4 * C], BF16) for e in range(E)]
         dc_slots = [tile(f"dc_slots{e}", [P, C, 4], BF16) for e in range(E)]
-        dc_planes = [tile(f"dc_planes{j}", [P, T], BF16) for j in range(4)]
+        dc_first = [tile(f"dc_first{j}", [P, T], BF16) for j in range(2)]
+        dc_planes = [dc_first[0][:], dc_first[1][:], da_slots[1][:, 0:T], da_slots[1][:, T:2 * T]]
         dh_sb = tile("dh_sb", [P, 4, T], F32)
 
-        for h in range(2):
+        def multiply_da(h):
             for th in range(2):
                 tok = slice(th * HALF, (th + 1) * HALF)
                 nc.vector.tensor_tensor(
-                    out=da_pairs[h][:, tok, :],
+                    out=da_pairs[h][:].rearrange("p (t i) -> p t i", i=2)[:, tok, :],
                     in0=dh_ps[h][th][:].rearrange("p i t -> p t i"),
                     in1=c_sb[:, 2 * h:2 * h + 2, tok].rearrange("p i t -> p t i"),
                     op=MULT,
                 )
-            window = da_pairs[h][:].rearrange("p t i -> p (t i)").bitcast(U32)
-            for e in range(E):
-                nc.vector.tensor_copy(out=da_got[e][:, h, :], in_=window.indirect(list_a[:, e * LC:(e + 1) * LC]))
+                nc.scalar.activation(out=dh_sb[:, 2 * h:2 * h + 2, tok], in_=dh_ps[h][th][:], func=COPY)
 
-        def products(name, slots, words, scales, e):
-            codes = tile(f"{name}_codes{e}", [P, C], U32)
+        def gather_da(h, e):
+            slots = da_slots[e][:].bitcast(U32).rearrange("p (s h) -> p s h", h=2)
+            nc.vector.tensor_copy(out=slots[:, :, h], in_=da_pairs[h][:].bitcast(U32).indirect(list_a[:, e * LC:(e + 1) * LC]))
+
+        def multiply_dc(j, pieces):
+            w = T // pieces
+            for i in range(pieces):
+                tok = slice(i * w, (i + 1) * w)
+                nc.gpsimd.tensor_tensor(out=dc_planes[j][:, tok], in0=dh_sb[:, j, tok], in1=a_sb[:, j, tok], op=MULT)
+
+        def products(name, slots, words, scales, e, codes_tag=None, res_tag=None):
+            codes = tile(f"{name}_codes{e}", [P, C], U32, codes_tag)
             codes_sc = tile(f"{name}_codes_sc{e}", [P, C], U8)
-            nc.vector.quantize_mx(out=codes[:].bitcast(FP8X4), scales=codes_sc[:], in_=slots[:].rearrange("p s j -> p (s j)"))
+            nc.vector.quantize_mx(out=codes[:].bitcast(FP8X4), scales=codes_sc[:], in_=slots)
             acc = ps.tile([P, 2, C], F32, name=f"{name}_ps{e}")
-            res = tile(f"{name}_sb{e}", [P, 2, C], F32)
+            res = [tile(f"{name}_sb{e}{kh}", [P, C], F32, res_tag if kh == 0 else None) for kh in range(2)]
             for kh in range(2):
                 nc.tensor.matmul_mx(
                     out=acc[:, kh, :],
@@ -142,39 +149,52 @@ def tile_moe_plb_none_kernel(
                     start=True, stop=True,
                 )
             for kh in range(2):
-                nc.scalar.activation(out=res[:, kh, :], in_=acc[:, kh, :], func=COPY)
+                nc.scalar.activation(out=res[kh][:], in_=acc[:, kh, :], func=COPY)
             return res
 
-        r_sb = []
-        for e in range(E):
-            nc.scalar.copy(
-                out=da_slots[e][:].rearrange("p s (h i) -> p s h i", h=2),
-                in_=da_got[e][:].bitcast(BF16).rearrange("p h (s i) -> p s h i", i=2),
-            )
-            r_sb.append(products("r", da_slots[e], wa, wa_sc, e))
+        def gather_dc(j, e):
+            nc.scalar.activation(out=dc_slots[e][:, :, j], in_=dc_planes[j].indirect(list_b[:, e * LC:(e + 1) * LC]), func=COPY)
 
-        for h in range(2):
-            for th in range(2):
-                nc.scalar.activation(out=dh_sb[:, 2 * h:2 * h + 2, th * HALF:(th + 1) * HALF], in_=dh_ps[h][th][:], func=COPY)
-        for j in range(4):
-            nc.gpsimd.tensor_tensor(out=dc_planes[j][:], in0=dh_sb[:, j, :], in1=a_sb[:, j, :], op=MULT)
+        def scatter(tok, res, lst, e):
+            nc.vector.tensor_copy(out=tok[:].indirect(lst[:, e * LC:(e + 1) * LC]), in_=res[:])
 
-        q_sb = []
-        for e in range(E):
-            for j in range(4):
-                nc.scalar.activation(out=dc_slots[e][:, :, j], in_=dc_planes[j][:].indirect(list_b[:, e * LC:(e + 1) * LC]), func=COPY)
-            q_sb.append(products("q", dc_slots[e], wb, wb_sc, e))
-
-        r_tok = [tile(f"r_tok{kh}", [P, T], F32) for kh in range(2)]
-        q_tok = [tile(f"q_tok{kh}", [P, T], F32) for kh in range(2)]
         total = [tile(f"total{kh}", [P, T], F32) for kh in range(2)]
-        for tok, res, lst in ((r_tok, r_sb, list_a), (q_tok, q_sb, list_b)):
+
+        multiply_da(0)
+        gather_da(0, 0)
+        gather_da(0, 1)
+        multiply_da(1)
+        gather_da(1, 0)
+        for j in range(2):
+            multiply_dc(j, 2)
             for e in range(E):
-                for kh in range(2):
-                    nc.vector.tensor_copy(out=tok[kh][:].indirect(lst[:, e * LC:(e + 1) * LC]), in_=res[e][:, kh, :])
-        nc.gpsimd.tensor_tensor(out=total[0][:], in0=r_tok[0][:], in1=q_tok[0][:], op=ADD)
+                gather_dc(j, e)
+        r0 = products("r", da_slots[0][:], wa, wa_sc, 0, None, "dc_first0")
+        gather_da(1, 1)
+        r1 = products("r", da_slots[1][:], wa, wa_sc, 1, None, "dc_first1")
+        multiply_dc(2, 1)
+        multiply_dc(3, 1)
+        r_tok0 = tile("r_tok0", [P, T], F32)
+        for j in range(2, 4):
+            gather_dc(j, 0)
+        scatter(r_tok0, r0[0], list_a, 0)
+        scatter(r_tok0, r1[0], list_a, 1)
+        q0 = products("q", dc_slots[0][:].rearrange("p s j -> p (s j)"), wb, wb_sc, 0)
+        for j in range(2, 4):
+            gather_dc(j, 1)
+        r_tok1 = tile("r_tok1", [P, T], F32, "dc_slots0")
+        scatter(r_tok1, r0[1], list_a, 0)
+        scatter(r_tok1, r1[1], list_a, 1)
+        q_tok0 = tile("q_tok0", [P, T], F32)
+        scatter(q_tok0, q0[0], list_b, 0)
+        q1 = products("q", dc_slots[1][:].rearrange("p s j -> p (s j)"), wb, wb_sc, 1, "q_sb00")
+        q_tok1 = tile("q_tok1", [P, T], F32, "dc_slots1")
+        scatter(q_tok1, q0[1], list_b, 0)
+        scatter(q_tok0, q1[0], list_b, 1)
+        nc.gpsimd.tensor_tensor(out=total[0][:], in0=r_tok0[:], in1=q_tok0[:], op=ADD)
         nc.sync.dma_start(out=out[0:P, :], in_=total[0][:])
+        scatter(q_tok1, q1[1], list_b, 1)
         for th in range(2):
             tok = slice(th * HALF, (th + 1) * HALF)
-            nc.vector.tensor_tensor(out=total[1][:, tok], in0=r_tok[1][:, tok], in1=q_tok[1][:, tok], op=ADD)
+            nc.vector.tensor_tensor(out=total[1][:, tok], in0=r_tok1[:, tok], in1=q_tok1[:, tok], op=ADD)
             (nc.scalar if th == 0 else nc.sync).dma_start(out=out[P:2 * P, tok], in_=total[1][:, tok])

@@ -46,16 +46,20 @@ def tile_moe_plb_none_kernel(
         wa_sc = tile("wa_sc", [P, E, K], U8)
         wb_sc = tile("wb_sc", [P, E, K], U8)
         c_sb = tile("c_sb", [P, 4, T], F32)
-        a_sb = tile("a_sb", [P, 4, T], F32)
+        a_lo = tile("a_lo", [P, 2, T], F32)
+        a_hi = tile("a_hi", [P, 2, T], F32)
 
         nc.vector.memset(w2_sc_raw[:].bitcast(I32), 0)
+        warm = tile("warm", [P, 2], F32)
+        nc.vector.memset(warm[:, 0:1], 0.0)
+        nc.scalar.activation(out=warm[:, 1:2], in_=warm[:, 0:1], func=COPY)
 
         def rows(q):
             return slice(32 * q, 32 * q + 4), slice(4 * q, 4 * q + 4)
 
-        def load_scales(eng, dst, src, q):
+        def load_scales(dst, src, q):
             part, row = rows(q)
-            eng.dma_start(out=dst[part, :].bitcast(I32), in_=src[0, row, :].bitcast(I32))
+            nc.sync.dma_start(out=dst[part, :].bitcast(I32), in_=src[0, row, :].bitcast(I32))
 
         def load_expert(words, scales, w_src, s_src):
             nc.sync.dma_start(out=words[:].bitcast(I32), in_=w_src[:, 0].rearrange("e p n -> p e n").bitcast(I32))
@@ -66,135 +70,150 @@ def tile_moe_plb_none_kernel(
         c_v = c.rearrange("(p j) t -> p j t", j=4)
         a_v = a.rearrange("(p j) t -> p j t", j=4)
         for q in range(2):
-            load_scales(nc.sync, dy_sc, dy_scales, q)
+            load_scales(dy_sc, dy_scales, q)
         nc.sync.dma_start(out=w2_raw[:].bitcast(I32), in_=w2t_words[0].bitcast(I32))
         nc.sync.dma_start(out=dy[:].bitcast(I32), in_=dy_words[0].rearrange("p t d -> p (t d)").bitcast(I32))
         for q in range(4):
-            load_scales(nc.sync, w2_sc_raw, w2t_scales, q)
+            load_scales(w2_sc_raw, w2t_scales, q)
         for q in range(2, 4):
-            load_scales(nc.sync, dy_sc, dy_scales, q)
-        for th in range(2):
-            nc.sync.dma_start(out=c_sb[:, 0:2, th * HALF:(th + 1) * HALF], in_=c_v[:, 0:2, th * HALF:(th + 1) * HALF])
+            load_scales(dy_sc, dy_scales, q)
+        for j in (2, 3):
+            nc.sync.dma_start(out=c_sb[:, j, :], in_=c_v[:, j, :])
         nc.sync.dma_start(list_a[:], offs)
-        nc.sync.dma_start(out=a_sb[:, 0:2, :], in_=a_v[:, 0:2, :])
-        nc.sync.dma_start(out=c_sb[:, 2:4, :], in_=c_v[:, 2:4, :])
-        nc.sync.dma_start(list_b[:], offs2)
+        nc.sync.dma_start(out=c_sb[:, 0:2, :], in_=c_v[:, 0:2, :])
         load_expert(wa, wa_sc, wat_words, wat_scales)
-        nc.sync.dma_start(out=a_sb[:, 2:4, :], in_=a_v[:, 2:4, :])
+        nc.sync.dma_start(out=a_lo[:], in_=a_v[:, 0:2, :])
+        nc.sync.dma_start(list_b[:], offs2)
+        nc.sync.dma_start(out=a_hi[:], in_=a_v[:, 2:4, :])
         load_expert(wb, wb_sc, wbt_words, wbt_scales)
 
         w2_in = w2_raw[:].bitcast(U16).rearrange("p (m j) -> p j m", j=4)
         w2_out = w2[:].bitcast(U16).rearrange("p (j m) -> p j m", j=4)
         sc_in = w2_sc_raw[:].rearrange("p (m j) -> p j m", j=4)
         sc_out = w2_sc[:].rearrange("p (j m) -> p j m", j=4)
+        for js in (slice(2, 4), slice(0, 2)):
+            nc.vector.tensor_copy(out=w2_out[:, js, :], in_=w2_in[:, js, :])
+            nc.vector.tensor_copy(out=sc_out[:, js, :], in_=sc_in[:, js, :])
 
-        dh_ps = [[ps.tile([P, 2, HALF], F32, name=f"dh_ps{h}{th}") for th in range(2)] for h in range(2)]
-        for h in range(2):
-            nc.vector.tensor_copy(out=sc_out[:, 2 * h:2 * h + 2, :], in_=sc_in[:, 2 * h:2 * h + 2, :])
-            nc.vector.tensor_copy(out=w2_out[:, 2 * h:2 * h + 2, :], in_=w2_in[:, 2 * h:2 * h + 2, :])
-        for h in range(2):
-            for th in range(2):
-                for i in range(2):
-                    j = 2 * h + i
-                    nc.tensor.matmul_mx(
-                        out=dh_ps[h][th][:, i, :],
-                        lhsT=w2[:, 2 * P * j:2 * P * (j + 1)].bitcast(FP4X4),
-                        lhsT_scale=w2_sc[:, P * j:P * (j + 1)],
-                        rhs=dy[:, th * HALF:(th + 1) * HALF].bitcast(FP8X4),
-                        rhs_scale=dy_sc[:, th * HALF:(th + 1) * HALF],
-                        start=True, stop=True,
-                    )
+        def first_product(dst, j, tok):
+            nc.tensor.matmul_mx(
+                out=dst,
+                lhsT=w2[:, 2 * P * j:2 * P * (j + 1)].bitcast(FP4X4),
+                lhsT_scale=w2_sc[:, P * j:P * (j + 1)],
+                rhs=dy[:, tok].bitcast(FP8X4),
+                rhs_scale=dy_sc[:, tok],
+                start=True, stop=True,
+            )
 
-        da_pairs = [tile(f"da_pairs{h}", [P, 2 * T], BF16) for h in range(2)]
-        da_slots = [tile(f"da_slots{e}", [P, 4 * C], BF16) for e in range(E)]
-        dc_slots = [tile(f"dc_slots{e}", [P, C, 4], BF16) for e in range(E)]
-        dc_first = [tile(f"dc_first{j}", [P, T], BF16) for j in range(2)]
-        dc_planes = [dc_first[0][:], dc_first[1][:], da_slots[1][:, 0:T], da_slots[1][:, T:2 * T]]
-        dh_sb = tile("dh_sb", [P, 4, T], F32)
+        halves = [slice(0, HALF), slice(HALF, T)]
+        dh_hi = [ps.tile([P, T], F32, name=f"dh_hi{i}") for i in range(2)]
+        dh_lo = [ps.tile([P, 2, HALF], F32, name=f"dh_lo{th}") for th in range(2)]
+        for i in range(2):
+            first_product(dh_hi[i][:], 2 + i, slice(0, T))
+        for th in range(2):
+            for j in range(2):
+                first_product(dh_lo[th][:, j, :], j, halves[th])
 
-        def multiply_da(h):
-            for th in range(2):
-                tok = slice(th * HALF, (th + 1) * HALF)
-                nc.vector.tensor_tensor(
-                    out=da_pairs[h][:].rearrange("p (t i) -> p t i", i=2)[:, tok, :],
-                    in0=dh_ps[h][th][:].rearrange("p i t -> p t i"),
-                    in1=c_sb[:, 2 * h:2 * h + 2, tok].rearrange("p i t -> p t i"),
-                    op=MULT,
-                )
-                nc.scalar.activation(out=dh_sb[:, 2 * h:2 * h + 2, tok], in_=dh_ps[h][th][:], func=COPY)
+        def slots_of(lst, e):
+            return lst[:, e * LC:(e + 1) * LC]
 
-        def gather_da(h, e):
-            slots = da_slots[e][:].bitcast(U32).rearrange("p (s h) -> p s h", h=2)
-            nc.vector.tensor_copy(out=slots[:, :, h], in_=da_pairs[h][:].bitcast(U32).indirect(list_a[:, e * LC:(e + 1) * LC]))
+        da_hi = tile("da_hi", [P, 2, T], BF16)
+        da_lo = tile("da_lo", [P, T, 2], BF16)
+        da_slots = tile("da_slots", [P, T, 4], BF16)
+        for i in range(2):
+            nc.vector.tensor_tensor(out=da_hi[:, i, :], in0=dh_hi[i][:], in1=c_sb[:, 2 + i, :], op=MULT)
+            for e in range(E):
+                nc.scalar.activation(out=da_slots[:, e * C:(e + 1) * C, 2 + i], in_=da_hi[:, i, :].indirect(slots_of(list_a, e)), func=COPY)
+        for th in range(2):
+            nc.vector.tensor_tensor(
+                out=da_lo[:, halves[th], :],
+                in0=dh_lo[th][:].rearrange("p j t -> p t j"),
+                in1=c_sb[:, 0:2, halves[th]].rearrange("p j t -> p t j"),
+                op=MULT,
+            )
+        pair_window = da_lo[:].rearrange("p t j -> p (t j)").bitcast(U32)
+        pair_slots = da_slots[:].rearrange("p s j -> p (s j)").bitcast(U32).rearrange("p (s h) -> p s h", h=2)
+        for e in range(E):
+            nc.vector.tensor_copy(out=pair_slots[:, e * C:(e + 1) * C, 0], in_=pair_window.indirect(slots_of(list_a, e)))
 
-        def multiply_dc(j, pieces):
-            w = T // pieces
-            for i in range(pieces):
-                tok = slice(i * w, (i + 1) * w)
-                nc.gpsimd.tensor_tensor(out=dc_planes[j][:, tok], in0=dh_sb[:, j, tok], in1=a_sb[:, j, tok], op=MULT)
+        dc_lo = tile("dc_lo", [P, 2, T], BF16, "da_lo")
+        for th in range(2):
+            nc.vector.tensor_tensor(out=dc_lo[:, :, halves[th]], in0=dh_lo[th][:], in1=a_lo[:, :, halves[th]], op=MULT)
 
-        def products(name, slots, words, scales, e, codes_tag=None, res_tag=None):
-            codes = tile(f"{name}_codes{e}", [P, C], U32, codes_tag)
-            codes_sc = tile(f"{name}_codes_sc{e}", [P, C], U8)
+        def quantize(name, slots, width, tag=None):
+            codes = tile(f"{name}_codes", [P, width], U32, tag)
+            codes_sc = tile(f"{name}_codes_sc", [P, width], U8)
             nc.vector.quantize_mx(out=codes[:].bitcast(FP8X4), scales=codes_sc[:], in_=slots)
-            acc = ps.tile([P, 2, C], F32, name=f"{name}_ps{e}")
-            res = [tile(f"{name}_sb{e}{kh}", [P, C], F32, res_tag if kh == 0 else None) for kh in range(2)]
-            for kh in range(2):
-                nc.tensor.matmul_mx(
-                    out=acc[:, kh, :],
-                    lhsT=words[:, e, 2 * P * kh:2 * P * (kh + 1)].bitcast(FP4X4),
-                    lhsT_scale=scales[:, e, P * kh:P * (kh + 1)],
-                    rhs=codes[:].bitcast(FP8X4),
-                    rhs_scale=codes_sc[:],
-                    start=True, stop=True,
-                )
-            for kh in range(2):
-                nc.scalar.activation(out=res[kh][:], in_=acc[:, kh, :], func=COPY)
-            return res
+            return codes, codes_sc
 
-        def gather_dc(j, e):
-            nc.scalar.activation(out=dc_slots[e][:, :, j], in_=dc_planes[j].indirect(list_b[:, e * LC:(e + 1) * LC]), func=COPY)
+        def expert_product(dst, words, scales, e, kh, codes, codes_sc):
+            nc.tensor.matmul_mx(
+                out=dst,
+                lhsT=words[:, e, 2 * P * kh:2 * P * (kh + 1)].bitcast(FP4X4),
+                lhsT_scale=scales[:, e, P * kh:P * (kh + 1)],
+                rhs=codes.bitcast(FP8X4),
+                rhs_scale=codes_sc,
+                start=True, stop=True,
+            )
+
+        def leave_psum(dst, src):
+            nc.scalar.activation(out=dst, in_=src, func=COPY)
 
         def scatter(tok, res, lst, e):
-            nc.vector.tensor_copy(out=tok[:].indirect(lst[:, e * LC:(e + 1) * LC]), in_=res[:])
+            nc.vector.tensor_copy(out=tok[:].indirect(slots_of(lst, e)), in_=res)
 
-        total = [tile(f"total{kh}", [P, T], F32) for kh in range(2)]
+        da_codes, da_codes_sc = quantize("da", da_slots[:].rearrange("p s j -> p (s j)"), T)
+        r_ps = [ps.tile([P, 2, C], F32, name=f"r_ps{e}") for e in range(E)]
+        for e in range(E):
+            for kh in range(2):
+                expert_product(r_ps[e][:, kh, :], wa, wa_sc, e, kh, da_codes[:, e * C:(e + 1) * C], da_codes_sc[:, e * C:(e + 1) * C])
+        r_sb = {}
+        for e, kh in ((0, 0), (0, 1), (1, 0)):
+            r_sb[e, kh] = tile(f"r_sb{e}{kh}", [P, C], F32)
+            leave_psum(r_sb[e, kh][:], r_ps[e][:, kh, :])
 
-        multiply_da(0)
-        gather_da(0, 0)
-        gather_da(0, 1)
-        multiply_da(1)
-        gather_da(1, 0)
-        for j in range(2):
-            multiply_dc(j, 2)
-            for e in range(E):
-                gather_dc(j, e)
-        r0 = products("r", da_slots[0][:], wa, wa_sc, 0, None, "dc_first0")
-        gather_da(1, 1)
-        r1 = products("r", da_slots[1][:], wa, wa_sc, 1, None, "dc_first1")
-        multiply_dc(2, 1)
-        multiply_dc(3, 1)
+        dc_hi = tile("dc_hi", [P, 2, T], BF16, "da_hi")
+        for i in range(2):
+            nc.vector.tensor_tensor(out=dc_hi[:, i, :], in0=dh_hi[i][:], in1=a_hi[:, i, :], op=MULT)
+        dc_planes = [dc_lo[:, 0, :], dc_lo[:, 1, :], dc_hi[:, 0, :], dc_hi[:, 1, :]]
+
+        def gather_dc(slots, e):
+            for j in range(4):
+                nc.scalar.activation(out=slots.rearrange("p (s j) -> p s j", j=4)[:, :, j], in_=dc_planes[j].indirect(slots_of(list_b, e)), func=COPY)
+
+        def second_pool(e, slots, tag=None):
+            codes, codes_sc = quantize(f"dc{e}", slots, C, tag)
+            q_ps = ps.tile([P, 2, C], F32, name=f"q_ps{e}")
+            q_sb = [tile(f"q_sb{e}{kh}", [P, C], F32) for kh in range(2)]
+            for kh in range(2):
+                expert_product(q_ps[:, kh, :], wb, wb_sc, e, kh, codes[:], codes_sc[:])
+            for kh in range(2):
+                leave_psum(q_sb[kh][:], q_ps[:, kh, :])
+            return q_sb
+
+        dc_slots0 = tile("dc_slots0", [P, 4 * C], BF16)
+        gather_dc(dc_slots0[:], 0)
+        r_sb[1, 1] = tile("r_sb11", [P, C], F32, "a_hi")
+        leave_psum(r_sb[1, 1][:], r_ps[1][:, 1, :])
         r_tok0 = tile("r_tok0", [P, T], F32)
-        for j in range(2, 4):
-            gather_dc(j, 0)
-        scatter(r_tok0, r0[0], list_a, 0)
-        scatter(r_tok0, r1[0], list_a, 1)
-        q0 = products("q", dc_slots[0][:].rearrange("p s j -> p (s j)"), wb, wb_sc, 0)
-        for j in range(2, 4):
-            gather_dc(j, 1)
-        r_tok1 = tile("r_tok1", [P, T], F32, "dc_slots0")
-        scatter(r_tok1, r0[1], list_a, 0)
-        scatter(r_tok1, r1[1], list_a, 1)
+        r_tok1 = tile("r_tok1", [P, T], F32)
+        scatter(r_tok0, r_sb[0, 0][:], list_a, 0)
+        dc_slots1 = tile("dc_slots1", [P, 4 * C], BF16, "r_sb00")
+        scatter(r_tok1, r_sb[0, 1][:], list_a, 0)
+        scatter(r_tok0, r_sb[1, 0][:], list_a, 1)
+        q0 = second_pool(0, dc_slots0[:])
+        gather_dc(dc_slots1[:], 1)
+        scatter(r_tok1, r_sb[1, 1][:], list_a, 1)
         q_tok0 = tile("q_tok0", [P, T], F32)
-        scatter(q_tok0, q0[0], list_b, 0)
-        q1 = products("q", dc_slots[1][:].rearrange("p s j -> p (s j)"), wb, wb_sc, 1, "q_sb00")
-        q_tok1 = tile("q_tok1", [P, T], F32, "dc_slots1")
-        scatter(q_tok1, q0[1], list_b, 0)
-        scatter(q_tok0, q1[0], list_b, 1)
+        scatter(q_tok0, q0[0][:], list_b, 0)
+        q1 = second_pool(1, dc_slots1[:])
+        q_tok1 = tile("q_tok1", [P, T], F32, "r_sb00")
+        scatter(q_tok1, q0[1][:], list_b, 0)
+        scatter(q_tok0, q1[0][:], list_b, 1)
+        total = [tile(f"total{kh}", [P, T], F32) for kh in range(2)]
         nc.gpsimd.tensor_tensor(out=total[0][:], in0=r_tok0[:], in1=q_tok0[:], op=ADD)
         nc.sync.dma_start(out=out[0:P, :], in_=total[0][:])
-        scatter(q_tok1, q1[1], list_b, 1)
+        scatter(q_tok1, q1[1][:], list_b, 1)
         for th in range(2):
-            tok = slice(th * HALF, (th + 1) * HALF)
-            nc.vector.tensor_tensor(out=total[1][:, tok], in0=r_tok1[:, tok], in1=q_tok1[:, tok], op=ADD)
-            (nc.scalar if th == 0 else nc.sync).dma_start(out=out[P:2 * P, tok], in_=total[1][:, tok])
+            nc.vector.tensor_tensor(out=total[1][:, halves[th]], in0=r_tok1[:, halves[th]], in1=q_tok1[:, halves[th]], op=ADD)
+            (nc.scalar if th == 0 else nc.sync).dma_start(out=out[P:2 * P, halves[th]], in_=total[1][:, halves[th]])

@@ -47,7 +47,7 @@ def tile_moe_plb_none_kernel(
         wb_sc = tile("wb_sc", [P, E, K], U8)
         c_sb = tile("c_sb", [P, 4, T], F32)
         a_lo = tile("a_lo", [P, 2, T], F32)
-        a_hi = tile("a_hi", [P, 2, T], F32)
+        a_hi = [tile(f"a_hi{i}", [P, T], F32) for i in range(2)]
 
         nc.vector.memset(w2_sc_raw[:].bitcast(I32), 0)
         warm = tile("warm", [P, 2], F32)
@@ -72,19 +72,20 @@ def tile_moe_plb_none_kernel(
         for q in range(2):
             load_scales(dy_sc, dy_scales, q)
         nc.sync.dma_start(out=w2_raw[:].bitcast(I32), in_=w2t_words[0].bitcast(I32))
-        nc.sync.dma_start(out=dy[:].bitcast(I32), in_=dy_words[0].rearrange("p t d -> p (t d)").bitcast(I32))
+        nc.gpsimd.dma_start(out=dy[:].bitcast(I32), in_=dy_words[0].rearrange("p t d -> p (t d)").bitcast(I32))
+        nc.sync.dma_start(out=c_sb[:, 2, :], in_=c_v[:, 2, :])
         for q in range(4):
             load_scales(w2_sc_raw, w2t_scales, q)
         for q in range(2, 4):
             load_scales(dy_sc, dy_scales, q)
-        for j in (2, 3):
-            nc.sync.dma_start(out=c_sb[:, j, :], in_=c_v[:, j, :])
+        nc.sync.dma_start(out=c_sb[:, 3, :], in_=c_v[:, 3, :])
         nc.sync.dma_start(list_a[:], offs)
         nc.sync.dma_start(out=c_sb[:, 0:2, :], in_=c_v[:, 0:2, :])
         load_expert(wa, wa_sc, wat_words, wat_scales)
         nc.sync.dma_start(out=a_lo[:], in_=a_v[:, 0:2, :])
         nc.sync.dma_start(list_b[:], offs2)
-        nc.sync.dma_start(out=a_hi[:], in_=a_v[:, 2:4, :])
+        for i in range(2):
+            nc.sync.dma_start(out=a_hi[i][:], in_=a_v[:, 2 + i, :])
         load_expert(wb, wb_sc, wbt_words, wbt_scales)
 
         w2_in = w2_raw[:].bitcast(U16).rearrange("p (m j) -> p j m", j=4)
@@ -106,7 +107,7 @@ def tile_moe_plb_none_kernel(
             )
 
         halves = [slice(0, HALF), slice(HALF, T)]
-        dh_hi = [ps.tile([P, T], F32, name=f"dh_hi{i}") for i in range(2)]
+        dh_hi = [ps.tile([P, T], F32, name=f"dh_hi{i}", tag=f"dh_hi{i}") for i in range(2)]
         dh_lo = [ps.tile([P, 2, HALF], F32, name=f"dh_lo{th}") for th in range(2)]
         for i in range(2):
             first_product(dh_hi[i][:], 2 + i, slice(0, T))
@@ -163,18 +164,22 @@ def tile_moe_plb_none_kernel(
             nc.vector.tensor_copy(out=tok[:].indirect(slots_of(lst, e)), in_=res)
 
         da_codes, da_codes_sc = quantize("da", da_slots[:].rearrange("p s j -> p (s j)"), T)
-        r_ps = [ps.tile([P, 2, C], F32, name=f"r_ps{e}") for e in range(E)]
-        for e in range(E):
-            for kh in range(2):
-                expert_product(r_ps[e][:, kh, :], wa, wa_sc, e, kh, da_codes[:, e * C:(e + 1) * C], da_codes_sc[:, e * C:(e + 1) * C])
+        def first_pool(dst, e, kh):
+            expert_product(dst, wa, wa_sc, e, kh, da_codes[:, e * C:(e + 1) * C], da_codes_sc[:, e * C:(e + 1) * C])
+
+        r_ps0 = ps.tile([P, 2, C], F32, name="r_ps0")
+        r_ps10 = ps.tile([P, C], F32, name="r_ps10")
+        r_src = {(0, 0): r_ps0[:, 0, :], (0, 1): r_ps0[:, 1, :], (1, 0): r_ps10[:]}
         r_sb = {}
-        for e, kh in ((0, 0), (0, 1), (1, 0)):
+        for e, kh in r_src:
+            first_pool(r_src[e, kh], e, kh)
+        for e, kh in r_src:
             r_sb[e, kh] = tile(f"r_sb{e}{kh}", [P, C], F32)
-            leave_psum(r_sb[e, kh][:], r_ps[e][:, kh, :])
+            leave_psum(r_sb[e, kh][:], r_src[e, kh])
 
         dc_hi = tile("dc_hi", [P, 2, T], BF16, "da_hi")
         for i in range(2):
-            nc.vector.tensor_tensor(out=dc_hi[:, i, :], in0=dh_hi[i][:], in1=a_hi[:, i, :], op=MULT)
+            nc.vector.tensor_tensor(out=dc_hi[:, i, :], in0=dh_hi[i][:], in1=a_hi[i][:], op=MULT)
         dc_planes = [dc_lo[:, 0, :], dc_lo[:, 1, :], dc_hi[:, 0, :], dc_hi[:, 1, :]]
 
         def gather_dc(slots, e):
@@ -193,10 +198,12 @@ def tile_moe_plb_none_kernel(
 
         dc_slots0 = tile("dc_slots0", [P, 4 * C], BF16)
         gather_dc(dc_slots0[:], 0)
-        r_sb[1, 1] = tile("r_sb11", [P, C], F32, "a_hi")
-        leave_psum(r_sb[1, 1][:], r_ps[1][:, 1, :])
-        r_tok0 = tile("r_tok0", [P, T], F32)
-        r_tok1 = tile("r_tok1", [P, T], F32)
+        r_ps11 = ps.tile([P, C], F32, name="r_ps11", tag="dh_hi1")
+        first_pool(r_ps11[:], 1, 1)
+        r_sb[1, 1] = tile("r_sb11", [P, C], F32)
+        leave_psum(r_sb[1, 1][:], r_ps11[:])
+        r_tok0 = tile("r_tok0", [P, T], F32, "a_hi1")
+        r_tok1 = tile("r_tok1", [P, T], F32, "a_hi0")
         scatter(r_tok0, r_sb[0, 0][:], list_a, 0)
         dc_slots1 = tile("dc_slots1", [P, 4 * C], BF16, "r_sb00")
         scatter(r_tok1, r_sb[0, 1][:], list_a, 0)

@@ -82,10 +82,10 @@ def tile_moe_plb_none_kernel(
         nc.sync.dma_start(list_a[:], offs)
         nc.sync.dma_start(out=c_sb[:, 0:2, :], in_=c_v[:, 0:2, :])
         load_expert(wa, wa_sc, wat_words, wat_scales)
-        nc.sync.dma_start(out=a_lo[:], in_=a_v[:, 0:2, :])
-        nc.sync.dma_start(list_b[:], offs2)
         for i in range(2):
             nc.sync.dma_start(out=a_hi[i][:], in_=a_v[:, 2 + i, :])
+        nc.sync.dma_start(out=a_lo[:], in_=a_v[:, 0:2, :])
+        nc.sync.dma_start(list_b[:], offs2)
         load_expert(wb, wb_sc, wbt_words, wbt_scales)
 
         w2_in = w2_raw[:].bitcast(U16).rearrange("p (m j) -> p j m", j=4)
@@ -137,9 +137,9 @@ def tile_moe_plb_none_kernel(
         for e in range(E):
             nc.vector.tensor_copy(out=pair_slots[:, e * C:(e + 1) * C, 0], in_=pair_window.indirect(slots_of(list_a, e)))
 
-        dc_lo = tile("dc_lo", [P, 2, T], BF16, "da_lo")
+        dh_lo_sb = tile("dh_lo_sb", [P, 2, T], F32)
         for th in range(2):
-            nc.vector.tensor_tensor(out=dc_lo[:, :, halves[th]], in0=dh_lo[th][:], in1=a_lo[:, :, halves[th]], op=MULT)
+            nc.scalar.activation(out=dh_lo_sb[:, :, halves[th]], in_=dh_lo[th][:], func=COPY)
 
         def quantize(name, slots, width, tag=None):
             codes = tile(f"{name}_codes", [P, width], U32, tag)
@@ -180,10 +180,13 @@ def tile_moe_plb_none_kernel(
         dc_hi = tile("dc_hi", [P, 2, T], BF16, "da_hi")
         for i in range(2):
             nc.vector.tensor_tensor(out=dc_hi[:, i, :], in0=dh_hi[i][:], in1=a_hi[i][:], op=MULT)
+        dc_lo = tile("dc_lo", [P, 2, T], BF16, "da_slots")
+        for j in range(2):
+            nc.gpsimd.tensor_tensor(out=dc_lo[:, j, :], in0=dh_lo_sb[:, j, :], in1=a_lo[:, j, :], op=MULT)
         dc_planes = [dc_lo[:, 0, :], dc_lo[:, 1, :], dc_hi[:, 0, :], dc_hi[:, 1, :]]
 
         def gather_dc(slots, e):
-            for j in range(4):
+            for j in (2, 3, 0, 1):
                 nc.scalar.activation(out=slots.rearrange("p (s j) -> p s j", j=4)[:, :, j], in_=dc_planes[j].indirect(slots_of(list_b, e)), func=COPY)
 
         def second_pool(e, slots, tag=None):
@@ -200,12 +203,12 @@ def tile_moe_plb_none_kernel(
         gather_dc(dc_slots0[:], 0)
         r_ps11 = ps.tile([P, C], F32, name="r_ps11", tag="dh_hi1")
         first_pool(r_ps11[:], 1, 1)
-        r_sb[1, 1] = tile("r_sb11", [P, C], F32)
+        r_sb[1, 1] = tile("r_sb11", [P, C], F32, "dh_lo_sb")
         leave_psum(r_sb[1, 1][:], r_ps11[:])
         r_tok0 = tile("r_tok0", [P, T], F32, "a_hi1")
         r_tok1 = tile("r_tok1", [P, T], F32, "a_hi0")
         scatter(r_tok0, r_sb[0, 0][:], list_a, 0)
-        dc_slots1 = tile("dc_slots1", [P, 4 * C], BF16, "r_sb00")
+        dc_slots1 = tile("dc_slots1", [P, 4 * C], BF16, "a_lo")
         scatter(r_tok1, r_sb[0, 1][:], list_a, 0)
         scatter(r_tok0, r_sb[1, 0][:], list_a, 1)
         q0 = second_pool(0, dc_slots0[:])
@@ -214,7 +217,7 @@ def tile_moe_plb_none_kernel(
         q_tok0 = tile("q_tok0", [P, T], F32)
         scatter(q_tok0, q0[0][:], list_b, 0)
         q1 = second_pool(1, dc_slots1[:])
-        q_tok1 = tile("q_tok1", [P, T], F32, "r_sb00")
+        q_tok1 = tile("q_tok1", [P, T], F32, "a_lo")
         scatter(q_tok1, q0[1][:], list_b, 0)
         scatter(q_tok0, q1[0][:], list_b, 1)
         total = [tile(f"total{kh}", [P, T], F32) for kh in range(2)]

@@ -45,11 +45,11 @@ def tile_moe_plb_none_kernel(
         wb = tile("wb", [P, E, 2 * K], U8)
         wa_sc = tile("wa_sc", [P, E, K], U8)
         wb_sc = tile("wb_sc", [P, E, K], U8)
-        c_sb = tile("c_sb", [P, 4, T], F32)
-        a_lo = tile("a_lo", [P, 2, T], F32)
-        a_hi = [tile(f"a_hi{i}", [P, T], F32) for i in range(2)]
+        c_hi = [tile(f"c_hi{i}", [P, T], F32) for i in range(2)]
+        c_lo = [tile(f"c_lo{th}", [P, 2, HALF], F32) for th in range(2)]
+        a_sb = [tile(f"a{j}", [P, T], F32) for j in range(4)]
+        halves = [slice(0, HALF), slice(HALF, T)]
 
-        nc.vector.memset(w2_sc_raw[:].bitcast(I32), 0)
         warm = tile("warm", [P, 2], F32)
         nc.vector.memset(warm[:, 0:1], 0.0)
         nc.scalar.activation(out=warm[:, 1:2], in_=warm[:, 0:1], func=COPY)
@@ -69,22 +69,24 @@ def tile_moe_plb_none_kernel(
 
         c_v = c.rearrange("(p j) t -> p j t", j=4)
         a_v = a.rearrange("(p j) t -> p j t", j=4)
+        for q in range(4):
+            nc.sync.dma_start(out=w2_sc_raw[32 * q:32 * q + 32, :].bitcast(I32), in_=w2t_scales[0, 4 * q:4 * q + 4, :].bitcast(I32).unsqueeze(0).to_broadcast([8, 4, H // 4]))
+        nc.sync.dma_start(out=w2_raw[:].bitcast(I32), in_=w2t_words[0].bitcast(I32))
         for q in range(2):
             load_scales(dy_sc, dy_scales, q)
-        nc.sync.dma_start(out=w2_raw[:].bitcast(I32), in_=w2t_words[0].bitcast(I32))
-        nc.gpsimd.dma_start(out=dy[:].bitcast(I32), in_=dy_words[0].rearrange("p t d -> p (t d)").bitcast(I32))
-        nc.sync.dma_start(out=c_sb[:, 2, :], in_=c_v[:, 2, :])
-        for q in range(4):
-            load_scales(w2_sc_raw, w2t_scales, q)
+        nc.sync.dma_start(out=dy[:].bitcast(I32), in_=dy_words[0].rearrange("p t d -> p (t d)").bitcast(I32))
         for q in range(2, 4):
             load_scales(dy_sc, dy_scales, q)
-        nc.sync.dma_start(out=c_sb[:, 3, :], in_=c_v[:, 3, :])
+        nc.sync.dma_start(out=c_hi[0][:], in_=c_v[:, 2, :])
         nc.sync.dma_start(list_a[:], offs)
-        nc.sync.dma_start(out=c_sb[:, 0:2, :], in_=c_v[:, 0:2, :])
+        nc.sync.dma_start(out=c_hi[1][:], in_=c_v[:, 3, :])
+        for th in range(2):
+            nc.sync.dma_start(out=c_lo[th][:], in_=c_v[:, 0:2, halves[th]])
+        for j in (2, 3):
+            nc.sync.dma_start(out=a_sb[j][:], in_=a_v[:, j, :])
         load_expert(wa, wa_sc, wat_words, wat_scales)
-        for i in range(2):
-            nc.sync.dma_start(out=a_hi[i][:], in_=a_v[:, 2 + i, :])
-        nc.sync.dma_start(out=a_lo[:], in_=a_v[:, 0:2, :])
+        for j in (0, 1):
+            nc.sync.dma_start(out=a_sb[j][:], in_=a_v[:, j, :])
         nc.sync.dma_start(list_b[:], offs2)
         load_expert(wb, wb_sc, wbt_words, wbt_scales)
 
@@ -93,8 +95,8 @@ def tile_moe_plb_none_kernel(
         sc_in = w2_sc_raw[:].rearrange("p (m j) -> p j m", j=4)
         sc_out = w2_sc[:].rearrange("p (j m) -> p j m", j=4)
         for js in (slice(2, 4), slice(0, 2)):
-            nc.vector.tensor_copy(out=w2_out[:, js, :], in_=w2_in[:, js, :])
             nc.vector.tensor_copy(out=sc_out[:, js, :], in_=sc_in[:, js, :])
+            nc.vector.tensor_copy(out=w2_out[:, js, :], in_=w2_in[:, js, :])
 
         def first_product(dst, j, tok):
             nc.tensor.matmul_mx(
@@ -106,7 +108,6 @@ def tile_moe_plb_none_kernel(
                 start=True, stop=True,
             )
 
-        halves = [slice(0, HALF), slice(HALF, T)]
         dh_hi = [ps.tile([P, T], F32, name=f"dh_hi{i}", tag=f"dh_hi{i}") for i in range(2)]
         dh_lo = [ps.tile([P, 2, HALF], F32, name=f"dh_lo{th}") for th in range(2)]
         for i in range(2):
@@ -115,115 +116,134 @@ def tile_moe_plb_none_kernel(
             for j in range(2):
                 first_product(dh_lo[th][:, j, :], j, halves[th])
 
-        def slots_of(lst, e):
-            return lst[:, e * LC:(e + 1) * LC]
-
-        da_hi = tile("da_hi", [P, 2, T], BF16)
-        da_lo = tile("da_lo", [P, T, 2], BF16)
-        da_slots = tile("da_slots", [P, T, 4], BF16)
-        for i in range(2):
-            nc.vector.tensor_tensor(out=da_hi[:, i, :], in0=dh_hi[i][:], in1=c_sb[:, 2 + i, :], op=MULT)
-            for e in range(E):
-                nc.scalar.activation(out=da_slots[:, e * C:(e + 1) * C, 2 + i], in_=da_hi[:, i, :].indirect(slots_of(list_a, e)), func=COPY)
-        for th in range(2):
-            nc.vector.tensor_tensor(
-                out=da_lo[:, halves[th], :],
-                in0=dh_lo[th][:].rearrange("p j t -> p t j"),
-                in1=c_sb[:, 0:2, halves[th]].rearrange("p j t -> p t j"),
-                op=MULT,
-            )
-        pair_window = da_lo[:].rearrange("p t j -> p (t j)").bitcast(U32)
-        pair_slots = da_slots[:].rearrange("p s j -> p (s j)").bitcast(U32).rearrange("p (s h) -> p s h", h=2)
-        for e in range(E):
-            nc.vector.tensor_copy(out=pair_slots[:, e * C:(e + 1) * C, 0], in_=pair_window.indirect(slots_of(list_a, e)))
-
-        dh_lo_sb = tile("dh_lo_sb", [P, 2, T], F32)
-        for th in range(2):
-            nc.scalar.activation(out=dh_lo_sb[:, :, halves[th]], in_=dh_lo[th][:], func=COPY)
-
-        def quantize(name, slots, width, tag=None):
-            codes = tile(f"{name}_codes", [P, width], U32, tag)
-            codes_sc = tile(f"{name}_codes_sc", [P, width], U8)
-            nc.vector.quantize_mx(out=codes[:].bitcast(FP8X4), scales=codes_sc[:], in_=slots)
-            return codes, codes_sc
-
-        def expert_product(dst, words, scales, e, kh, codes, codes_sc):
-            nc.tensor.matmul_mx(
-                out=dst,
-                lhsT=words[:, e, 2 * P * kh:2 * P * (kh + 1)].bitcast(FP4X4),
-                lhsT_scale=scales[:, e, P * kh:P * (kh + 1)],
-                rhs=codes.bitcast(FP8X4),
-                rhs_scale=codes_sc,
-                start=True, stop=True,
-            )
+        def slots_of(lst, first, count):
+            return lst[:, first // 16:(first + count) // 16]
 
         def leave_psum(dst, src):
             nc.scalar.activation(out=dst, in_=src, func=COPY)
 
-        def scatter(tok, res, lst, e):
-            nc.vector.tensor_copy(out=tok[:].indirect(slots_of(lst, e)), in_=res)
+        def gather_plane(slots, j, plane, offsets):
+            nc.scalar.activation(out=slots[:].rearrange("p (s j) -> p s j", j=4)[:, :, j], in_=plane.indirect(offsets), func=COPY)
 
-        da_codes, da_codes_sc = quantize("da", da_slots[:].rearrange("p s j -> p (s j)"), T)
-        def first_pool(dst, e, kh):
-            expert_product(dst, wa, wa_sc, e, kh, da_codes[:, e * C:(e + 1) * C], da_codes_sc[:, e * C:(e + 1) * C])
+        def quantize(name, slots, width, tag=None):
+            codes = tile(f"{name}_codes", [P, width], U32, tag)
+            codes_sc = tile(f"{name}_codes_sc", [P, width], U8)
+            nc.vector.quantize_mx(out=codes[:].bitcast(FP8X4), scales=codes_sc[:], in_=slots[:])
+            return codes, codes_sc
 
-        r_ps0 = ps.tile([P, 2, C], F32, name="r_ps0")
-        r_ps10 = ps.tile([P, C], F32, name="r_ps10")
-        r_src = {(0, 0): r_ps0[:, 0, :], (0, 1): r_ps0[:, 1, :], (1, 0): r_ps10[:]}
-        r_sb = {}
-        for e, kh in r_src:
-            first_pool(r_src[e, kh], e, kh)
-        for e, kh in r_src:
-            r_sb[e, kh] = tile(f"r_sb{e}{kh}", [P, C], F32)
-            leave_psum(r_sb[e, kh][:], r_src[e, kh])
+        def expert_product(dst, words, scales, e, kh, quantized):
+            nc.tensor.matmul_mx(
+                out=dst,
+                lhsT=words[:, e, 2 * P * kh:2 * P * (kh + 1)].bitcast(FP4X4),
+                lhsT_scale=scales[:, e, P * kh:P * (kh + 1)],
+                rhs=quantized[0][:].bitcast(FP8X4),
+                rhs_scale=quantized[1][:],
+                start=True, stop=True,
+            )
 
-        dc_hi = tile("dc_hi", [P, 2, T], BF16, "da_hi")
+        def scatter(tok, res, lst, first, count):
+            nc.vector.tensor_copy(out=tok[:].indirect(slots_of(lst, first, count)), in_=res)
+
+        da_hi = [tile(f"da_hi{i}", [P, T], BF16) for i in range(2)]
+        da_lo = tile("da_lo", [P, T, 2], BF16)
+        da_slots = [tile(f"da_slots{e}", [P, 4 * C], BF16) for e in range(E)]
         for i in range(2):
-            nc.vector.tensor_tensor(out=dc_hi[:, i, :], in0=dh_hi[i][:], in1=a_hi[i][:], op=MULT)
-        dc_lo = tile("dc_lo", [P, 2, T], BF16, "da_slots")
-        for j in range(2):
-            nc.gpsimd.tensor_tensor(out=dc_lo[:, j, :], in0=dh_lo_sb[:, j, :], in1=a_lo[:, j, :], op=MULT)
-        dc_planes = [dc_lo[:, 0, :], dc_lo[:, 1, :], dc_hi[:, 0, :], dc_hi[:, 1, :]]
-
-        def gather_dc(slots, e):
-            for j in (2, 3, 0, 1):
-                nc.scalar.activation(out=slots.rearrange("p (s j) -> p s j", j=4)[:, :, j], in_=dc_planes[j].indirect(slots_of(list_b, e)), func=COPY)
-
-        def second_pool(e, slots, tag=None):
-            codes, codes_sc = quantize(f"dc{e}", slots, C, tag)
-            q_ps = ps.tile([P, 2, C], F32, name=f"q_ps{e}")
-            q_sb = [tile(f"q_sb{e}{kh}", [P, C], F32) for kh in range(2)]
-            for kh in range(2):
-                expert_product(q_ps[:, kh, :], wb, wb_sc, e, kh, codes[:], codes_sc[:])
-            for kh in range(2):
-                leave_psum(q_sb[kh][:], q_ps[:, kh, :])
-            return q_sb
-
-        dc_slots0 = tile("dc_slots0", [P, 4 * C], BF16)
-        gather_dc(dc_slots0[:], 0)
-        r_ps11 = ps.tile([P, C], F32, name="r_ps11", tag="dh_hi1")
-        first_pool(r_ps11[:], 1, 1)
-        r_sb[1, 1] = tile("r_sb11", [P, C], F32, "dh_lo_sb")
-        leave_psum(r_sb[1, 1][:], r_ps11[:])
-        r_tok0 = tile("r_tok0", [P, T], F32, "a_hi1")
-        r_tok1 = tile("r_tok1", [P, T], F32, "a_hi0")
-        scatter(r_tok0, r_sb[0, 0][:], list_a, 0)
-        dc_slots1 = tile("dc_slots1", [P, 4 * C], BF16, "a_lo")
-        scatter(r_tok1, r_sb[0, 1][:], list_a, 0)
-        scatter(r_tok0, r_sb[1, 0][:], list_a, 1)
-        q0 = second_pool(0, dc_slots0[:])
-        gather_dc(dc_slots1[:], 1)
-        scatter(r_tok1, r_sb[1, 1][:], list_a, 1)
-        q_tok0 = tile("q_tok0", [P, T], F32)
-        scatter(q_tok0, q0[0][:], list_b, 0)
-        q1 = second_pool(1, dc_slots1[:])
-        q_tok1 = tile("q_tok1", [P, T], F32, "a_lo")
-        scatter(q_tok1, q0[1][:], list_b, 0)
-        scatter(q_tok0, q1[0][:], list_b, 1)
-        total = [tile(f"total{kh}", [P, T], F32) for kh in range(2)]
-        nc.gpsimd.tensor_tensor(out=total[0][:], in0=r_tok0[:], in1=q_tok0[:], op=ADD)
-        nc.sync.dma_start(out=out[0:P, :], in_=total[0][:])
-        scatter(q_tok1, q1[1][:], list_b, 1)
+            nc.vector.tensor_tensor(out=da_hi[i][:], in0=dh_hi[i][:], in1=c_hi[i][:], op=MULT)
         for th in range(2):
-            nc.vector.tensor_tensor(out=total[1][:, halves[th]], in0=r_tok1[:, halves[th]], in1=q_tok1[:, halves[th]], op=ADD)
+            nc.vector.tensor_tensor(
+                out=da_lo[:, halves[th], :],
+                in0=dh_lo[th][:].rearrange("p j t -> p t j"),
+                in1=c_lo[th][:].rearrange("p j t -> p t j"),
+                op=MULT,
+            )
+        dh2_sb = tile("dh2_sb", [P, T], F32)
+        leave_psum(dh2_sb[:], dh_hi[0][:])
+        dc = {2: tile("dc2", [P, T], BF16)}
+        nc.gpsimd.tensor_tensor(out=dc[2][:], in0=dh2_sb[:], in1=a_sb[2][:], op=MULT)
+        pair_window = da_lo[:].rearrange("p t j -> p (t j)").bitcast(U32)
+        for e in range(E):
+            for i in range(2):
+                gather_plane(da_slots[e], 2 + i, da_hi[i][:], slots_of(list_a, e * C, C))
+
+        def gather_pairs(e):
+            pair_slots = da_slots[e][:].bitcast(U32).rearrange("p (s h) -> p s h", h=2)
+            nc.vector.tensor_copy(out=pair_slots[:, :, 0], in_=pair_window.indirect(slots_of(list_a, e * C, C)))
+
+        gather_pairs(0)
+        dc[3] = tile("dc3", [P, T], BF16, "c_lo1")
+        nc.vector.tensor_tensor(out=dc[3][:], in0=dh_hi[1][:], in1=a_sb[3][:], op=MULT)
+        da_q = [quantize("da0", da_slots[0], C)]
+        gather_pairs(1)
+        da_q.append(quantize("da1", da_slots[1], C))
+        r_ps = {}
+        for e in range(E):
+            for kh in range(2):
+                r_ps[e, kh] = ps.tile([P, C], F32, name=f"r_ps{e}{kh}", tag=f"r_ps{e}{kh}")
+                expert_product(r_ps[e, kh][:], wa, wa_sc, e, kh, da_q[e])
+
+        r_sb = {key: tile(f"r_sb{key[0]}{key[1]}", [P, C], F32) for key in ((0, 0), (0, 1), (1, 0))}
+        r_tok = [tile(f"r_tok{kh}", [P, T], F32) for kh in range(2)]
+        leave_psum(r_sb[0, 0][:], r_ps[0, 0][:])
+        scatter(r_tok[0], r_sb[0, 0][:], list_a, 0, C)
+        dh_lo_sb = tile("dh_lo_sb", [P, 2, T], F32, "da0_codes")
+        for th in range(2):
+            leave_psum(dh_lo_sb[:, :, halves[th]], dh_lo[th][:])
+        for j in range(2):
+            dc[j] = tile(f"dc{j}", [P, T], BF16)
+            nc.gpsimd.tensor_tensor(out=dc[j][:], in0=dh_lo_sb[:, j, :], in1=a_sb[j][:], op=MULT)
+        leave_psum(r_sb[0, 1][:], r_ps[0, 1][:])
+        scatter(r_tok[1], r_sb[0, 1][:], list_a, 0, C)
+
+        dc_slots0 = tile("dc_slots0", [P, 4 * C], BF16, "da0_codes_sc")
+        gather_plane(dc_slots0, 2, dc[2][:], slots_of(list_b, 0, C))
+        leave_psum(r_sb[1, 0][:], r_ps[1, 0][:])
+        scatter(r_tok[0], r_sb[1, 0][:], list_a, C, C)
+        gather_plane(dc_slots0, 3, dc[3][:], slots_of(list_b, 0, C))
+        r_sb11a = tile("r_sb11a", [P, P], F32)
+        leave_psum(r_sb11a[:], r_ps[1, 1][:, 0:P])
+        scatter(r_tok[1], r_sb11a[:], list_a, C, P)
+        for j in range(2):
+            gather_plane(dc_slots0, j, dc[j][:], slots_of(list_b, 0, C))
+        dc_q0 = quantize("dc0", dc_slots0, C)
+        r_sb11b = tile("r_sb11b", [P, P], F32, "da0_codes")
+        leave_psum(r_sb11b[:], r_ps[1, 1][:, P:C])
+        scatter(r_tok[1], r_sb11b[:], list_a, C + P, P)
+
+        q_ps0 = [ps.tile([P, C], F32, name=f"q_ps0{kh}", tag=f"r_ps0{kh}") for kh in range(2)]
+        for kh in range(2):
+            expert_product(q_ps0[kh][:], wb, wb_sc, 0, kh, dc_q0)
+        q_sb00 = tile("q_sb00", [P, C], F32)
+        q_sb01 = [tile(f"q_sb01{u}", [P, P], F32) for u in range(2)]
+        q_tok0 = tile("q_tok0", [P, T], F32)
+        q_tok1 = tile("q_tok1", [P, T], F32)
+        leave_psum(q_sb00[:], q_ps0[0][:])
+        scatter(q_tok0, q_sb00[:], list_b, 0, C)
+        for u in range(2):
+            leave_psum(q_sb01[u][:], q_ps0[1][:, u * P:(u + 1) * P])
+
+        dc_slots1 = [tile("dc_slots1a", [P, 4 * P], BF16, "a1"), tile("dc_slots1b", [P, 4 * P], BF16, "dc0_codes_sc")]
+        for u in range(2):
+            for j in (2, 3, 0, 1):
+                gather_plane(dc_slots1[u], j, dc[j][:], slots_of(list_b, C + u * P, P))
+        scatter(q_tok1, q_sb01[0][:], list_b, 0, P)
+        dc_q1a = quantize("dc1a", dc_slots1[0], P, "q_sb00")
+        scatter(q_tok1, q_sb01[1][:], list_b, P, P)
+        dc_q1 = [dc_q1a, quantize("dc1b", dc_slots1[1], P, "q_sb010")]
+        q_ps10 = [ps.tile([P, P], F32, name="q_ps10a", tag="r_ps10"), ps.tile([P, P], F32, name="q_ps10b", tag="dh_hi0")]
+        q_ps11 = ps.tile([P, C], F32, name="q_ps11", tag="r_ps11")
+        for u in range(2):
+            expert_product(q_ps10[u][:], wb, wb_sc, 1, 0, dc_q1[u])
+            expert_product(q_ps11[:, u * P:(u + 1) * P], wb, wb_sc, 1, 1, dc_q1[u])
+        for u in range(2):
+            q_sb10 = tile(f"q_sb10{u}", [P, P], F32)
+            leave_psum(q_sb10[:], q_ps10[u][:])
+            scatter(q_tok0, q_sb10[:], list_b, C + u * P, P)
+        q_sb11 = tile("q_sb11", [P, C], F32)
+        leave_psum(q_sb11[:], q_ps11[:])
+        total = [tile(f"total{kh}", [P, T], F32) for kh in range(2)]
+        nc.gpsimd.tensor_tensor(out=total[0][:], in0=r_tok[0][:], in1=q_tok0[:], op=ADD)
+        nc.sync.dma_start(out=out[0:P, :], in_=total[0][:])
+        scatter(q_tok1, q_sb11[:], list_b, C, C)
+        for th in range(2):
+            nc.vector.tensor_tensor(out=total[1][:, halves[th]], in0=r_tok[1][:, halves[th]], in1=q_tok1[:, halves[th]], op=ADD)
             (nc.scalar if th == 0 else nc.sync).dma_start(out=out[P:2 * P, halves[th]], in_=total[1][:, halves[th]])

@@ -47,7 +47,8 @@ def tile_moe_plb_none_kernel(
         wb_sc = tile("wb_sc", [P, E, K], U8)
         c_hi = [tile(f"c_hi{i}", [P, T], F32) for i in range(2)]
         c_lo = [tile(f"c_lo{th}", [P, 2, HALF], F32) for th in range(2)]
-        a_sb = [tile(f"a{j}", [P, T], F32) for j in range(4)]
+        a_hi = [tile(f"a_hi{i}", [P, T], F32) for i in range(2)]
+        a_lo = [tile(f"a_lo{th}", [P, 2, HALF], F32) for th in range(2)]
         halves = [slice(0, HALF), slice(HALF, T)]
 
         warm = tile("warm", [P, 2], F32)
@@ -77,16 +78,16 @@ def tile_moe_plb_none_kernel(
         nc.sync.dma_start(out=dy[:].bitcast(I32), in_=dy_words[0].rearrange("p t d -> p (t d)").bitcast(I32))
         for q in range(2, 4):
             load_scales(dy_sc, dy_scales, q)
-        nc.sync.dma_start(out=c_hi[0][:], in_=c_v[:, 2, :])
         nc.sync.dma_start(list_a[:], offs)
+        nc.sync.dma_start(out=c_hi[0][:], in_=c_v[:, 2, :])
         nc.sync.dma_start(out=c_hi[1][:], in_=c_v[:, 3, :])
         for th in range(2):
             nc.sync.dma_start(out=c_lo[th][:], in_=c_v[:, 0:2, halves[th]])
-        for j in (2, 3):
-            nc.sync.dma_start(out=a_sb[j][:], in_=a_v[:, j, :])
+        for i in range(2):
+            nc.sync.dma_start(out=a_hi[i][:], in_=a_v[:, 2 + i, :])
         load_expert(wa, wa_sc, wat_words, wat_scales)
-        for j in (0, 1):
-            nc.sync.dma_start(out=a_sb[j][:], in_=a_v[:, j, :])
+        for th in range(2):
+            nc.sync.dma_start(out=a_lo[th][:], in_=a_v[:, 0:2, halves[th]])
         nc.sync.dma_start(list_b[:], offs2)
         load_expert(wb, wb_sc, wbt_words, wbt_scales)
 
@@ -146,7 +147,7 @@ def tile_moe_plb_none_kernel(
 
         da_hi = [tile(f"da_hi{i}", [P, T], BF16) for i in range(2)]
         da_lo = tile("da_lo", [P, T, 2], BF16)
-        da_slots = [tile(f"da_slots{e}", [P, 4 * C], BF16) for e in range(E)]
+        da_slots = [tile("da_slots0", [P, 4 * C], BF16), tile("da_slots1", [P, 4 * C], BF16, "c_hi1")]
         for i in range(2):
             nc.vector.tensor_tensor(out=da_hi[i][:], in0=dh_hi[i][:], in1=c_hi[i][:], op=MULT)
         for th in range(2):
@@ -156,10 +157,6 @@ def tile_moe_plb_none_kernel(
                 in1=c_lo[th][:].rearrange("p j t -> p t j"),
                 op=MULT,
             )
-        dh2_sb = tile("dh2_sb", [P, T], F32)
-        leave_psum(dh2_sb[:], dh_hi[0][:])
-        dc = {2: tile("dc2", [P, T], BF16)}
-        nc.gpsimd.tensor_tensor(out=dc[2][:], in0=dh2_sb[:], in1=a_sb[2][:], op=MULT)
         pair_window = da_lo[:].rearrange("p t j -> p (t j)").bitcast(U32)
         for e in range(E):
             for i in range(2):
@@ -169,12 +166,12 @@ def tile_moe_plb_none_kernel(
             pair_slots = da_slots[e][:].bitcast(U32).rearrange("p (s h) -> p s h", h=2)
             nc.vector.tensor_copy(out=pair_slots[:, :, 0], in_=pair_window.indirect(slots_of(list_a, e * C, C)))
 
-        gather_pairs(0)
-        dc[3] = tile("dc3", [P, T], BF16, "c_lo1")
-        nc.vector.tensor_tensor(out=dc[3][:], in0=dh_hi[1][:], in1=a_sb[3][:], op=MULT)
-        da_q = [quantize("da0", da_slots[0], C)]
-        gather_pairs(1)
-        da_q.append(quantize("da1", da_slots[1], C))
+        for e in range(E):
+            gather_pairs(e)
+        da_q = [quantize(f"da{e}", da_slots[e], C) for e in range(E)]
+        dc_hi = tile("dc_hi", [P, 2, T], BF16, "da_slots0")
+        for i in range(2):
+            nc.vector.tensor_tensor(out=dc_hi[:, i, :], in0=dh_hi[i][:], in1=a_hi[i][:], op=MULT)
         r_ps = {}
         for e in range(E):
             for kh in range(2):
@@ -183,67 +180,67 @@ def tile_moe_plb_none_kernel(
 
         r_sb = {key: tile(f"r_sb{key[0]}{key[1]}", [P, C], F32) for key in ((0, 0), (0, 1), (1, 0))}
         r_tok = [tile(f"r_tok{kh}", [P, T], F32) for kh in range(2)]
+        dc_lo = tile("dc_lo", [P, 2, T], BF16)
+        dc = [dc_lo[:, 0, :], dc_lo[:, 1, :], dc_hi[:, 0, :], dc_hi[:, 1, :]]
+
+        def low_planes_of_dc(th, tag=None):
+            dh_sb = tile(f"dh_lo_sb{th}", [P, 2, HALF], F32, tag)
+            leave_psum(dh_sb[:], dh_lo[th][:])
+            nc.gpsimd.tensor_tensor(out=dc_lo[:, :, halves[th]], in0=dh_sb[:], in1=a_lo[th][:], op=MULT)
+
+        low_planes_of_dc(0)
         leave_psum(r_sb[0, 0][:], r_ps[0, 0][:])
         scatter(r_tok[0], r_sb[0, 0][:], list_a, 0, C)
-        dh_lo_sb = tile("dh_lo_sb", [P, 2, T], F32, "da0_codes")
-        for th in range(2):
-            leave_psum(dh_lo_sb[:, :, halves[th]], dh_lo[th][:])
-        for j in range(2):
-            dc[j] = tile(f"dc{j}", [P, T], BF16)
-            nc.gpsimd.tensor_tensor(out=dc[j][:], in0=dh_lo_sb[:, j, :], in1=a_sb[j][:], op=MULT)
+        low_planes_of_dc(1, "da0_codes")
         leave_psum(r_sb[0, 1][:], r_ps[0, 1][:])
         scatter(r_tok[1], r_sb[0, 1][:], list_a, 0, C)
 
         dc_slots0 = tile("dc_slots0", [P, 4 * C], BF16, "da0_codes_sc")
-        gather_plane(dc_slots0, 2, dc[2][:], slots_of(list_b, 0, C))
+        gather_plane(dc_slots0, 2, dc[2], slots_of(list_b, 0, C))
         leave_psum(r_sb[1, 0][:], r_ps[1, 0][:])
         scatter(r_tok[0], r_sb[1, 0][:], list_a, C, C)
-        gather_plane(dc_slots0, 3, dc[3][:], slots_of(list_b, 0, C))
-        r_sb11a = tile("r_sb11a", [P, P], F32)
-        leave_psum(r_sb11a[:], r_ps[1, 1][:, 0:P])
-        scatter(r_tok[1], r_sb11a[:], list_a, C, P)
+        gather_plane(dc_slots0, 3, dc[3], slots_of(list_b, 0, C))
         for j in range(2):
-            gather_plane(dc_slots0, j, dc[j][:], slots_of(list_b, 0, C))
+            gather_plane(dc_slots0, j, dc[j], slots_of(list_b, 0, C))
         dc_q0 = quantize("dc0", dc_slots0, C)
-        r_sb11b = tile("r_sb11b", [P, P], F32, "da0_codes")
-        leave_psum(r_sb11b[:], r_ps[1, 1][:, P:C])
-        scatter(r_tok[1], r_sb11b[:], list_a, C + P, P)
+        r_sb11 = tile("r_sb11", [P, C], F32, "da0_codes")
+        leave_psum(r_sb11[:], r_ps[1, 1][:])
+        scatter(r_tok[1], r_sb11[:], list_a, C, C)
 
         q_ps0 = [ps.tile([P, C], F32, name=f"q_ps0{kh}", tag=f"r_ps0{kh}") for kh in range(2)]
         for kh in range(2):
             expert_product(q_ps0[kh][:], wb, wb_sc, 0, kh, dc_q0)
-        q_sb00 = tile("q_sb00", [P, C], F32)
-        q_sb01 = [tile(f"q_sb01{u}", [P, P], F32) for u in range(2)]
         q_tok0 = tile("q_tok0", [P, T], F32)
         q_tok1 = tile("q_tok1", [P, T], F32)
-        leave_psum(q_sb00[:], q_ps0[0][:])
-        scatter(q_tok0, q_sb00[:], list_b, 0, C)
-        for u in range(2):
-            leave_psum(q_sb01[u][:], q_ps0[1][:, u * P:(u + 1) * P])
+        q_sb0a = [tile(f"q_sb0a{kh}", [P, P], F32) for kh in range(2)]
+        for kh in range(2):
+            leave_psum(q_sb0a[kh][:], q_ps0[kh][:, 0:P])
 
-        dc_slots1 = [tile("dc_slots1a", [P, 4 * P], BF16, "a1"), tile("dc_slots1b", [P, 4 * P], BF16, "dc0_codes_sc")]
+        dc_slots1 = [tile("dc_slots1a", [P, 4 * P], BF16, "a_lo1"), tile("dc_slots1b", [P, 4 * P], BF16, "dc0_codes_sc")]
         for u in range(2):
-            for j in (2, 3, 0, 1):
-                gather_plane(dc_slots1[u], j, dc[j][:], slots_of(list_b, C + u * P, P))
-        scatter(q_tok1, q_sb01[0][:], list_b, 0, P)
-        dc_q1a = quantize("dc1a", dc_slots1[0], P, "q_sb00")
-        scatter(q_tok1, q_sb01[1][:], list_b, P, P)
-        dc_q1 = [dc_q1a, quantize("dc1b", dc_slots1[1], P, "q_sb010")]
-        q_ps10 = [ps.tile([P, P], F32, name="q_ps10a", tag="r_ps10"), ps.tile([P, P], F32, name="q_ps10b", tag="dh_hi0")]
-        q_ps11 = ps.tile([P, C], F32, name="q_ps11", tag="r_ps11")
+            for j in (2, 0, 3, 1):
+                gather_plane(dc_slots1[u], j, dc[j], slots_of(list_b, C + u * P, P))
+        q_sb0b = tile("q_sb0b", [P, 2, P], F32, "dc_lo")
+        for kh in range(2):
+            leave_psum(q_sb0b[:, kh, :], q_ps0[kh][:, P:C])
+        scatter(q_tok0, q_sb0a[0][:], list_b, 0, P)
+        scatter(q_tok1, q_sb0a[1][:], list_b, 0, P)
+        dc_q1 = (tile("dc1_codes", [P, C], U32, "q_sb0a0"), tile("dc1_codes_sc", [P, C], U8))
         for u in range(2):
-            expert_product(q_ps10[u][:], wb, wb_sc, 1, 0, dc_q1[u])
-            expert_product(q_ps11[:, u * P:(u + 1) * P], wb, wb_sc, 1, 1, dc_q1[u])
-        for u in range(2):
-            q_sb10 = tile(f"q_sb10{u}", [P, P], F32)
-            leave_psum(q_sb10[:], q_ps10[u][:])
-            scatter(q_tok0, q_sb10[:], list_b, C + u * P, P)
-        q_sb11 = tile("q_sb11", [P, C], F32)
-        leave_psum(q_sb11[:], q_ps11[:])
+            cols = slice(u * P, (u + 1) * P)
+            nc.vector.quantize_mx(out=dc_q1[0][:, cols].bitcast(FP8X4), scales=dc_q1[1][:, cols], in_=dc_slots1[u][:])
+        scatter(q_tok0, q_sb0b[:, 0, :], list_b, P, P)
+        scatter(q_tok1, q_sb0b[:, 1, :], list_b, P, P)
+        q_sb1 = [tile(f"q_sb1{kh}", [P, C], F32) for kh in range(2)]
+        for kh in range(2):
+            q_ps1 = ps.tile([P, C], F32, name=f"q_ps1{kh}", tag=f"r_ps1{kh}")
+            expert_product(q_ps1[:], wb, wb_sc, 1, kh, dc_q1)
+            leave_psum(q_sb1[kh][:], q_ps1[:])
+        scatter(q_tok0, q_sb1[0][:], list_b, C, C)
         total = [tile(f"total{kh}", [P, T], F32) for kh in range(2)]
         nc.gpsimd.tensor_tensor(out=total[0][:], in0=r_tok[0][:], in1=q_tok0[:], op=ADD)
         nc.sync.dma_start(out=out[0:P, :], in_=total[0][:])
-        scatter(q_tok1, q_sb11[:], list_b, C, C)
+        scatter(q_tok1, q_sb1[1][:], list_b, C, C)
         for th in range(2):
             nc.vector.tensor_tensor(out=total[1][:, halves[th]], in0=r_tok[1][:, halves[th]], in1=q_tok1[:, halves[th]], op=ADD)
             (nc.scalar if th == 0 else nc.sync).dma_start(out=out[P:2 * P, halves[th]], in_=total[1][:, halves[th]])

@@ -70,19 +70,19 @@ def tile_moe_plb_none_kernel(
 
         c_v = c.rearrange("(p j) t -> p j t", j=4)
         a_v = a.rearrange("(p j) t -> p j t", j=4)
+        for q in range(2):
+            load_scales(dy_sc, dy_scales, q)
         for q in range(4):
             nc.sync.dma_start(out=w2_sc_raw[32 * q:32 * q + 32, :].bitcast(I32), in_=w2t_scales[0, 4 * q:4 * q + 4, :].bitcast(I32).unsqueeze(0).to_broadcast([8, 4, H // 4]))
         nc.sync.dma_start(out=w2_raw[:].bitcast(I32), in_=w2t_words[0].bitcast(I32))
-        for q in range(2):
-            load_scales(dy_sc, dy_scales, q)
         nc.sync.dma_start(out=dy[:].bitcast(I32), in_=dy_words[0].rearrange("p t d -> p (t d)").bitcast(I32))
         for q in range(2, 4):
             load_scales(dy_sc, dy_scales, q)
         nc.sync.dma_start(list_a[:], offs)
         nc.sync.dma_start(out=c_hi[0][:], in_=c_v[:, 2, :])
-        nc.sync.dma_start(out=c_hi[1][:], in_=c_v[:, 3, :])
         for th in range(2):
             nc.sync.dma_start(out=c_lo[th][:], in_=c_v[:, 0:2, halves[th]])
+        nc.sync.dma_start(out=c_hi[1][:], in_=c_v[:, 3, :])
         for i in range(2):
             nc.sync.dma_start(out=a_hi[i][:], in_=a_v[:, 2 + i, :])
         load_expert(wa, wa_sc, wat_words, wat_scales)
@@ -111,11 +111,11 @@ def tile_moe_plb_none_kernel(
 
         dh_hi = [ps.tile([P, T], F32, name=f"dh_hi{i}", tag=f"dh_hi{i}") for i in range(2)]
         dh_lo = [ps.tile([P, 2, HALF], F32, name=f"dh_lo{th}") for th in range(2)]
-        for i in range(2):
-            first_product(dh_hi[i][:], 2 + i, slice(0, T))
+        first_product(dh_hi[0][:], 2, slice(0, T))
         for th in range(2):
             for j in range(2):
                 first_product(dh_lo[th][:, j, :], j, halves[th])
+        first_product(dh_hi[1][:], 3, slice(0, T))
 
         def slots_of(lst, first, count):
             return lst[:, first // 16:(first + count) // 16]
@@ -147,9 +147,8 @@ def tile_moe_plb_none_kernel(
 
         da_hi = [tile(f"da_hi{i}", [P, T], BF16) for i in range(2)]
         da_lo = tile("da_lo", [P, T, 2], BF16)
-        da_slots = [tile("da_slots0", [P, 4 * C], BF16), tile("da_slots1", [P, 4 * C], BF16, "c_hi1")]
-        for i in range(2):
-            nc.vector.tensor_tensor(out=da_hi[i][:], in0=dh_hi[i][:], in1=c_hi[i][:], op=MULT)
+        da_slots = [tile(f"da_slots{e}", [P, 4 * C], BF16) for e in range(E)]
+        nc.vector.tensor_tensor(out=da_hi[0][:], in0=dh_hi[0][:], in1=c_hi[0][:], op=MULT)
         for th in range(2):
             nc.vector.tensor_tensor(
                 out=da_lo[:, halves[th], :],
@@ -157,21 +156,22 @@ def tile_moe_plb_none_kernel(
                 in1=c_lo[th][:].rearrange("p j t -> p t j"),
                 op=MULT,
             )
+        nc.vector.tensor_tensor(out=da_hi[1][:], in0=dh_hi[1][:], in1=c_hi[1][:], op=MULT)
         pair_window = da_lo[:].rearrange("p t j -> p (t j)").bitcast(U32)
-        for e in range(E):
-            for i in range(2):
+        for i in range(2):
+            for e in range(E):
                 gather_plane(da_slots[e], 2 + i, da_hi[i][:], slots_of(list_a, e * C, C))
 
         def gather_pairs(e):
             pair_slots = da_slots[e][:].bitcast(U32).rearrange("p (s h) -> p s h", h=2)
             nc.vector.tensor_copy(out=pair_slots[:, :, 0], in_=pair_window.indirect(slots_of(list_a, e * C, C)))
 
+        dc_hi = tile("dc_hi", [P, 2, T], BF16, "c_hi1")
+        da_q = []
         for e in range(E):
             gather_pairs(e)
-        da_q = [quantize(f"da{e}", da_slots[e], C) for e in range(E)]
-        dc_hi = tile("dc_hi", [P, 2, T], BF16, "da_slots0")
-        for i in range(2):
-            nc.vector.tensor_tensor(out=dc_hi[:, i, :], in0=dh_hi[i][:], in1=a_hi[i][:], op=MULT)
+            nc.vector.tensor_tensor(out=dc_hi[:, e, :], in0=dh_hi[e][:], in1=a_hi[e][:], op=MULT)
+            da_q.append(quantize(f"da{e}", da_slots[e], C))
         r_ps = {}
         for e in range(E):
             for kh in range(2):
@@ -188,7 +188,7 @@ def tile_moe_plb_none_kernel(
             leave_psum(dh_sb[:], dh_lo[th][:])
             nc.gpsimd.tensor_tensor(out=dc_lo[:, :, halves[th]], in0=dh_sb[:], in1=a_lo[th][:], op=MULT)
 
-        low_planes_of_dc(0)
+        low_planes_of_dc(0, "da_hi1")
         leave_psum(r_sb[0, 0][:], r_ps[0, 0][:])
         scatter(r_tok[0], r_sb[0, 0][:], list_a, 0, C)
         low_planes_of_dc(1, "da0_codes")

@@ -51,6 +51,7 @@ def tile_moe_plb_none_kernel(
         a_lo = [tile(f"a_lo{th}", [P, 2, HALF], F32) for th in range(2)]
         halves = [slice(0, HALF), slice(HALF, T)]
 
+        nc.vector.memset(w2_sc_raw[:].bitcast(I32), 0)
         warm = tile("warm", [P, 2], F32)
         nc.vector.memset(warm[:, 0:1], 0.0)
         nc.scalar.activation(out=warm[:, 1:2], in_=warm[:, 0:1], func=COPY)
@@ -72,14 +73,14 @@ def tile_moe_plb_none_kernel(
         a_v = a.rearrange("(p j) t -> p j t", j=4)
         for q in range(2):
             load_scales(dy_sc, dy_scales, q)
-        for q in range(4):
-            nc.sync.dma_start(out=w2_sc_raw[32 * q:32 * q + 32, :].bitcast(I32), in_=w2t_scales[0, 4 * q:4 * q + 4, :].bitcast(I32).unsqueeze(0).to_broadcast([8, 4, H // 4]))
         nc.sync.dma_start(out=w2_raw[:].bitcast(I32), in_=w2t_words[0].bitcast(I32))
+        for q in range(4):
+            load_scales(w2_sc_raw, w2t_scales, q)
         nc.sync.dma_start(out=dy[:].bitcast(I32), in_=dy_words[0].rearrange("p t d -> p (t d)").bitcast(I32))
         for q in range(2, 4):
             load_scales(dy_sc, dy_scales, q)
-        nc.sync.dma_start(list_a[:], offs)
         nc.sync.dma_start(out=c_hi[0][:], in_=c_v[:, 2, :])
+        nc.sync.dma_start(list_a[:], offs)
         for th in range(2):
             nc.sync.dma_start(out=c_lo[th][:], in_=c_v[:, 0:2, halves[th]])
         nc.sync.dma_start(out=c_hi[1][:], in_=c_v[:, 3, :])

@@ -47,8 +47,8 @@ def tile_moe_plb_none_kernel(
         wb_sc = tile("wb_sc", [P, E, K], U8)
         c_hi = [tile(f"c_hi{i}", [P, T], F32) for i in range(2)]
         c_lo = [tile(f"c_lo{th}", [P, 2, HALF], F32) for th in range(2)]
-        a_hi = [tile(f"a_hi{i}", [P, T], F32) for i in range(2)]
-        a_lo = [tile(f"a_lo{th}", [P, 2, HALF], F32) for th in range(2)]
+        a_hi = tile("a_hi", [P, 2, T], F32)
+        a_lo = tile("a_lo", [P, 2, T], F32)
         halves = [slice(0, HALF), slice(HALF, T)]
 
         nc.vector.memset(w2_sc_raw[:].bitcast(I32), 0)
@@ -84,11 +84,9 @@ def tile_moe_plb_none_kernel(
         for th in range(2):
             nc.sync.dma_start(out=c_lo[th][:], in_=c_v[:, 0:2, halves[th]])
         nc.sync.dma_start(out=c_hi[1][:], in_=c_v[:, 3, :])
-        for i in range(2):
-            nc.sync.dma_start(out=a_hi[i][:], in_=a_v[:, 2 + i, :])
+        nc.sync.dma_start(out=a_hi[:], in_=a_v[:, 2:4, :])
         load_expert(wa, wa_sc, wat_words, wat_scales)
-        for th in range(2):
-            nc.sync.dma_start(out=a_lo[th][:], in_=a_v[:, 0:2, halves[th]])
+        nc.sync.dma_start(out=a_lo[:], in_=a_v[:, 0:2, :])
         nc.sync.dma_start(list_b[:], offs2)
         load_expert(wb, wb_sc, wbt_words, wbt_scales)
 
@@ -171,7 +169,7 @@ def tile_moe_plb_none_kernel(
         da_q = []
         for e in range(E):
             gather_pairs(e)
-            nc.vector.tensor_tensor(out=dc_hi[:, e, :], in0=dh_hi[e][:], in1=a_hi[e][:], op=MULT)
+            nc.vector.tensor_tensor(out=dc_hi[:, e, :], in0=dh_hi[e][:], in1=a_hi[:, e, :], op=MULT)
             da_q.append(quantize(f"da{e}", da_slots[e], C))
         r_ps = {}
         for e in range(E):
@@ -187,7 +185,7 @@ def tile_moe_plb_none_kernel(
         def low_planes_of_dc(th, tag=None):
             dh_sb = tile(f"dh_lo_sb{th}", [P, 2, HALF], F32, tag)
             leave_psum(dh_sb[:], dh_lo[th][:])
-            nc.gpsimd.tensor_tensor(out=dc_lo[:, :, halves[th]], in0=dh_sb[:], in1=a_lo[th][:], op=MULT)
+            nc.gpsimd.tensor_tensor(out=dc_lo[:, :, halves[th]], in0=dh_sb[:], in1=a_lo[:, :, halves[th]], op=MULT)
 
         low_planes_of_dc(0, "da_hi1")
         leave_psum(r_sb[0, 0][:], r_ps[0, 0][:])
@@ -217,7 +215,7 @@ def tile_moe_plb_none_kernel(
         for kh in range(2):
             leave_psum(q_sb0a[kh][:], q_ps0[kh][:, 0:P])
 
-        dc_slots1 = [tile("dc_slots1a", [P, 4 * P], BF16, "a_lo1"), tile("dc_slots1b", [P, 4 * P], BF16, "dc0_codes_sc")]
+        dc_slots1 = [tile("dc_slots1a", [P, 4 * P], BF16, "a_lo"), tile("dc_slots1b", [P, 4 * P], BF16, "dc0_codes_sc")]
         for u in range(2):
             for j in (2, 0, 3, 1):
                 gather_plane(dc_slots1[u], j, dc[j], slots_of(list_b, C + u * P, P))

@@ -120,7 +120,7 @@ def tile_moe_plb_none_kernel(
             return lst[:, first // 16:(first + count) // 16]
 
         def leave_psum(dst, src):
-            nc.scalar.activation(out=dst, in_=src, func=COPY)
+            nc.scalar.copy(out=dst, in_=src)
 
         def gather_plane(slots, j, plane, offsets):
             nc.scalar.activation(out=slots[:].rearrange("p (s j) -> p s j", j=4)[:, :, j], in_=plane.indirect(offsets), func=COPY)
@@ -150,9 +150,9 @@ def tile_moe_plb_none_kernel(
         nc.vector.tensor_tensor(out=da_hi[0][:], in0=dh_hi[0][:], in1=c_hi[0][:], op=MULT)
         for th in range(2):
             nc.vector.tensor_tensor(
-                out=da_lo[:, halves[th], :],
-                in0=dh_lo[th][:].rearrange("p j t -> p t j"),
-                in1=c_lo[th][:].rearrange("p j t -> p t j"),
+                out=da_lo[:, halves[th], :].rearrange("p (g i) j -> p g j i", i=4),
+                in0=dh_lo[th][:].rearrange("p j (g i) -> p g j i", i=4),
+                in1=c_lo[th][:].rearrange("p j (g i) -> p g j i", i=4),
                 op=MULT,
             )
         nc.vector.tensor_tensor(out=da_hi[1][:], in0=dh_hi[1][:], in1=c_hi[1][:], op=MULT)

@@ -19,7 +19,6 @@ ADD = mybir.AluOpType.add
 COPY = mybir.ActivationFunctionType.Copy
 P = 128
 HALF = 256
-LC = C // 16
 
 
 def tile_moe_plb_none_kernel(
@@ -33,6 +32,9 @@ def tile_moe_plb_none_kernel(
         def tile(name, shape, dtype, tag=None):
             return sb.tile(shape, dtype, name=name, tag=tag or name, align_bytes=64)
 
+        def bank(name, shape, tag=None):
+            return ps.tile(shape, F32, name=name, tag=tag or name)
+
         list_a = tile("list_a", [P, T // 16], U16)
         list_b = tile("list_b", [P, T // 16], U16)
         w2_raw = tile("w2_raw", [P, 2 * H], U8)
@@ -45,11 +47,10 @@ def tile_moe_plb_none_kernel(
         wb = tile("wb", [P, E, 2 * K], U8)
         wa_sc = tile("wa_sc", [P, E, K], U8)
         wb_sc = tile("wb_sc", [P, E, K], U8)
-        c_hi = [tile(f"c_hi{i}", [P, T], F32) for i in range(2)]
-        c_lo = [tile(f"c_lo{th}", [P, 2, HALF], F32) for th in range(2)]
-        a_hi = tile("a_hi", [P, 2, T], F32)
-        a_lo = tile("a_lo", [P, 2, T], F32)
         halves = [slice(0, HALF), slice(HALF, T)]
+        parts = [(h, th) for h in range(2) for th in range(2)]
+        c_sb = {k: tile(f"c{k[0]}{k[1]}", [P, 2, HALF], F32) for k in parts}
+        a_sb = {k: tile(f"a{k[0]}{k[1]}", [P, 2, HALF], F32) for k in parts}
 
         nc.vector.memset(w2_sc_raw[:].bitcast(I32), 0)
         warm = tile("warm", [P, 2], F32)
@@ -69,8 +70,10 @@ def tile_moe_plb_none_kernel(
                 part, row = rows(q)
                 nc.sync.dma_start(out=scales[part].bitcast(I32), in_=s_src[:, 0, row, :].rearrange("e r n -> r e n").bitcast(I32))
 
-        c_v = c.rearrange("(p j) t -> p j t", j=4)
-        a_v = a.rearrange("(p j) t -> p j t", j=4)
+        def load_part(dst, src, key):
+            h, th = key
+            nc.sync.dma_start(out=dst[key][:], in_=src.rearrange("(p j) t -> p j t", j=4)[:, 2 * h:2 * h + 2, halves[th]])
+
         for q in range(2):
             load_scales(dy_sc, dy_scales, q)
         nc.sync.dma_start(out=w2_raw[:].bitcast(I32), in_=w2t_words[0].bitcast(I32))
@@ -79,14 +82,14 @@ def tile_moe_plb_none_kernel(
         nc.sync.dma_start(out=dy[:].bitcast(I32), in_=dy_words[0].rearrange("p t d -> p (t d)").bitcast(I32))
         for q in range(2, 4):
             load_scales(dy_sc, dy_scales, q)
-        nc.sync.dma_start(out=c_hi[0][:], in_=c_v[:, 2, :])
+        for key in parts:
+            load_part(c_sb, c, key)
         nc.sync.dma_start(list_a[:], offs)
-        for th in range(2):
-            nc.sync.dma_start(out=c_lo[th][:], in_=c_v[:, 0:2, halves[th]])
-        nc.sync.dma_start(out=c_hi[1][:], in_=c_v[:, 3, :])
-        nc.sync.dma_start(out=a_hi[:], in_=a_v[:, 2:4, :])
+        for key in parts[:2]:
+            load_part(a_sb, a, key)
         load_expert(wa, wa_sc, wat_words, wat_scales)
-        nc.sync.dma_start(out=a_lo[:], in_=a_v[:, 0:2, :])
+        for key in parts[2:]:
+            load_part(a_sb, a, key)
         nc.sync.dma_start(list_b[:], offs2)
         load_expert(wb, wb_sc, wbt_words, wbt_scales)
 
@@ -94,36 +97,31 @@ def tile_moe_plb_none_kernel(
         w2_out = w2[:].bitcast(U16).rearrange("p (j m) -> p j m", j=4)
         sc_in = w2_sc_raw[:].rearrange("p (m j) -> p j m", j=4)
         sc_out = w2_sc[:].rearrange("p (j m) -> p j m", j=4)
-        for js in (slice(2, 4), slice(0, 2)):
+        for js in (slice(0, 2), slice(2, 4)):
             nc.vector.tensor_copy(out=sc_out[:, js, :], in_=sc_in[:, js, :])
             nc.vector.tensor_copy(out=w2_out[:, js, :], in_=w2_in[:, js, :])
 
-        def first_product(dst, j, tok):
-            nc.tensor.matmul_mx(
-                out=dst,
-                lhsT=w2[:, 2 * P * j:2 * P * (j + 1)].bitcast(FP4X4),
-                lhsT_scale=w2_sc[:, P * j:P * (j + 1)],
-                rhs=dy[:, tok].bitcast(FP8X4),
-                rhs_scale=dy_sc[:, tok],
-                start=True, stop=True,
-            )
-
-        dh_hi = [ps.tile([P, T], F32, name=f"dh_hi{i}", tag=f"dh_hi{i}") for i in range(2)]
-        dh_lo = [ps.tile([P, 2, HALF], F32, name=f"dh_lo{th}") for th in range(2)]
-        first_product(dh_hi[0][:], 2, slice(0, T))
-        for th in range(2):
-            for j in range(2):
-                first_product(dh_lo[th][:, j, :], j, halves[th])
-        first_product(dh_hi[1][:], 3, slice(0, T))
+        dh = {}
+        for h, th in parts:
+            dh[h, th] = bank(f"dh{h}{th}", [P, 2, HALF])
+            for i in range(2):
+                j = 2 * h + i
+                nc.tensor.matmul_mx(
+                    out=dh[h, th][:, i, :],
+                    lhsT=w2[:, 2 * P * j:2 * P * (j + 1)].bitcast(FP4X4),
+                    lhsT_scale=w2_sc[:, P * j:P * (j + 1)],
+                    rhs=dy[:, halves[th]].bitcast(FP8X4),
+                    rhs_scale=dy_sc[:, halves[th]],
+                    start=True, stop=True,
+                )
 
         def slots_of(lst, first, count):
             return lst[:, first // 16:(first + count) // 16]
 
-        def leave_psum(dst, src):
-            nc.scalar.copy(out=dst, in_=src)
-
-        def gather_plane(slots, j, plane, offsets):
-            nc.scalar.activation(out=slots[:].rearrange("p (s j) -> p s j", j=4)[:, :, j], in_=plane.indirect(offsets), func=COPY)
+        def gather_pairs(slots, h, pairs, lst, first, count):
+            words = slots[:].bitcast(U32).rearrange("p (s h) -> p s h", h=2)
+            window = pairs[:].rearrange("p t j -> p (t j)").bitcast(U32)
+            nc.vector.tensor_copy(out=words[:, :, h], in_=window.indirect(slots_of(lst, first, count)))
 
         def quantize(name, slots, width, tag=None):
             codes = tile(f"{name}_codes", [P, width], U32, tag)
@@ -141,105 +139,78 @@ def tile_moe_plb_none_kernel(
                 start=True, stop=True,
             )
 
-        def scatter(tok, res, lst, first, count):
-            nc.vector.tensor_copy(out=tok[:].indirect(slots_of(lst, first, count)), in_=res)
+        def leave_psum_s(name, src, tag=None):
+            dst = tile(name, [P, C], F32, tag)
+            nc.scalar.copy(out=dst[:], in_=src[:])
+            return dst
 
-        da_hi = [tile(f"da_hi{i}", [P, T], BF16) for i in range(2)]
-        da_lo = tile("da_lo", [P, T, 2], BF16)
-        da_slots = [tile(f"da_slots{e}", [P, 4 * C], BF16) for e in range(E)]
-        nc.vector.tensor_tensor(out=da_hi[0][:], in0=dh_hi[0][:], in1=c_hi[0][:], op=MULT)
-        for th in range(2):
+        def leave_psum_v(name, src, tag=None):
+            dst = tile(name, [P, C], F32, tag)
+            nc.vector.tensor_copy(out=dst[:], in_=src[:])
+            return dst
+
+        def scatter_v(tok, res, lst, e):
+            nc.vector.tensor_copy(out=tok[:].indirect(slots_of(lst, e * C, C)), in_=res[:])
+
+        def scatter_s(tok, res, lst, e):
+            nc.scalar.activation(out=tok[:].indirect(slots_of(lst, e * C, C)), in_=res[:], func=COPY)
+
+        da = [tile(f"da{h}", [P, T, 2], BF16) for h in range(2)]
+        dc = [tile(f"dc{h}", [P, T, 2], BF16) for h in range(2)]
+
+        def product_v(dst, saved, h, th):
             nc.vector.tensor_tensor(
-                out=da_lo[:, halves[th], :].rearrange("p (g i) j -> p g j i", i=4),
-                in0=dh_lo[th][:].rearrange("p j (g i) -> p g j i", i=4),
-                in1=c_lo[th][:].rearrange("p j (g i) -> p g j i", i=4),
+                out=dst[h][:, halves[th], :].rearrange("p (g i) j -> p g j i", i=4),
+                in0=dh[h, th][:].rearrange("p j (g i) -> p g j i", i=4),
+                in1=saved[h, th][:].rearrange("p j (g i) -> p g j i", i=4),
                 op=MULT,
             )
-        nc.vector.tensor_tensor(out=da_hi[1][:], in0=dh_hi[1][:], in1=c_hi[1][:], op=MULT)
-        pair_window = da_lo[:].rearrange("p t j -> p (t j)").bitcast(U32)
-        for i in range(2):
-            for e in range(E):
-                gather_plane(da_slots[e], 2 + i, da_hi[i][:], slots_of(list_a, e * C, C))
 
-        def gather_pairs(e):
-            pair_slots = da_slots[e][:].bitcast(U32).rearrange("p (s h) -> p s h", h=2)
-            nc.vector.tensor_copy(out=pair_slots[:, :, 0], in_=pair_window.indirect(slots_of(list_a, e * C, C)))
+        for h, th in parts:
+            product_v(da, c_sb, h, th)
+        for h, th in parts[:3]:
+            dh_sb = tile(f"dh_sb{h}{th}", [P, HALF, 2], F32)
+            nc.scalar.copy(out=dh_sb[:], in_=dh[h, th][:].rearrange("p j t -> p t j"))
+            nc.gpsimd.tensor_tensor(out=dc[h][:, halves[th], :], in0=dh_sb[:], in1=a_sb[h, th][:].rearrange("p j t -> p t j"), op=MULT)
 
-        dc_hi = tile("dc_hi", [P, 2, T], BF16, "c_hi1")
-        da_q = []
-        for e in range(E):
-            gather_pairs(e)
-            nc.vector.tensor_tensor(out=dc_hi[:, e, :], in0=dh_hi[e][:], in1=a_hi[:, e, :], op=MULT)
-            da_q.append(quantize(f"da{e}", da_slots[e], C))
         r_ps = {}
         for e in range(E):
+            slots = tile(f"da_slots{e}", [P, 4 * C], BF16)
+            for h in range(2):
+                gather_pairs(slots, h, da[h], list_a, e * C, C)
+            quantized = quantize(f"da_q{e}", slots, C)
             for kh in range(2):
-                r_ps[e, kh] = ps.tile([P, C], F32, name=f"r_ps{e}{kh}", tag=f"r_ps{e}{kh}")
-                expert_product(r_ps[e, kh][:], wa, wa_sc, e, kh, da_q[e])
+                r_ps[e, kh] = bank(f"r_ps{e}{kh}", [P, C])
+                expert_product(r_ps[e, kh][:], wa, wa_sc, e, kh, quantized)
 
-        r_sb = {key: tile(f"r_sb{key[0]}{key[1]}", [P, C], F32) for key in ((0, 0), (0, 1), (1, 0))}
         r_tok = [tile(f"r_tok{kh}", [P, T], F32) for kh in range(2)]
-        dc_lo = tile("dc_lo", [P, 2, T], BF16)
-        dc = [dc_lo[:, 0, :], dc_lo[:, 1, :], dc_hi[:, 0, :], dc_hi[:, 1, :]]
+        q_tok = [tile(f"q_tok{kh}", [P, T], F32) for kh in range(2)]
+        scatter_s(r_tok[0], leave_psum_s("r_sb00", r_ps[0, 0]), list_a, 0)
+        scatter_s(r_tok[0], leave_psum_s("r_sb10", r_ps[1, 0]), list_a, 1)
+        scatter_s(r_tok[1], leave_psum_s("r_sb01", r_ps[0, 1]), list_a, 0)
 
-        def low_planes_of_dc(th, tag=None):
-            dh_sb = tile(f"dh_lo_sb{th}", [P, 2, HALF], F32, tag)
-            leave_psum(dh_sb[:], dh_lo[th][:])
-            nc.gpsimd.tensor_tensor(out=dc_lo[:, :, halves[th]], in0=dh_sb[:], in1=a_lo[:, :, halves[th]], op=MULT)
+        product_v(dc, a_sb, *parts[3])
+        dc_slots = [tile(f"dc_slots{e}", [P, 4 * C], BF16) for e in range(E)]
+        for e in range(E):
+            gather_pairs(dc_slots[e], 0, dc[0], list_b, e * C, C)
+        q_ps = {}
+        for e in range(E):
+            gather_pairs(dc_slots[e], 1, dc[1], list_b, e * C, C)
+            quantized = quantize(f"dc_q{e}", dc_slots[e], C)
+            for kh in range(2):
+                q_ps[e, kh] = bank(f"q_ps{e}{kh}", [P, C], f"dh{e}{kh}")
+                expert_product(q_ps[e, kh][:], wb, wb_sc, e, kh, quantized)
 
-        low_planes_of_dc(0, "da_hi1")
-        leave_psum(r_sb[0, 0][:], r_ps[0, 0][:])
-        scatter(r_tok[0], r_sb[0, 0][:], list_a, 0, C)
-        low_planes_of_dc(1, "da0_codes")
-        leave_psum(r_sb[0, 1][:], r_ps[0, 1][:])
-        scatter(r_tok[1], r_sb[0, 1][:], list_a, 0, C)
-
-        dc_slots0 = tile("dc_slots0", [P, 4 * C], BF16, "da0_codes_sc")
-        gather_plane(dc_slots0, 2, dc[2], slots_of(list_b, 0, C))
-        leave_psum(r_sb[1, 0][:], r_ps[1, 0][:])
-        scatter(r_tok[0], r_sb[1, 0][:], list_a, C, C)
-        gather_plane(dc_slots0, 3, dc[3], slots_of(list_b, 0, C))
-        for j in range(2):
-            gather_plane(dc_slots0, j, dc[j], slots_of(list_b, 0, C))
-        dc_q0 = quantize("dc0", dc_slots0, C)
-        r_sb11 = tile("r_sb11", [P, C], F32, "da0_codes")
-        leave_psum(r_sb11[:], r_ps[1, 1][:])
-        scatter(r_tok[1], r_sb11[:], list_a, C, C)
-
-        q_ps0 = [ps.tile([P, C], F32, name=f"q_ps0{kh}", tag=f"r_ps0{kh}") for kh in range(2)]
-        for kh in range(2):
-            expert_product(q_ps0[kh][:], wb, wb_sc, 0, kh, dc_q0)
-        q_tok0 = tile("q_tok0", [P, T], F32)
-        q_tok1 = tile("q_tok1", [P, T], F32)
-        q_sb0a = [tile(f"q_sb0a{kh}", [P, P], F32) for kh in range(2)]
-        for kh in range(2):
-            leave_psum(q_sb0a[kh][:], q_ps0[kh][:, 0:P])
-
-        dc_slots1 = [tile("dc_slots1a", [P, 4 * P], BF16, "a_lo"), tile("dc_slots1b", [P, 4 * P], BF16, "dc0_codes_sc")]
-        for u in range(2):
-            for j in (2, 0, 3, 1):
-                gather_plane(dc_slots1[u], j, dc[j], slots_of(list_b, C + u * P, P))
-        q_sb0b = tile("q_sb0b", [P, 2, P], F32, "dc_lo")
-        for kh in range(2):
-            leave_psum(q_sb0b[:, kh, :], q_ps0[kh][:, P:C])
-        scatter(q_tok0, q_sb0a[0][:], list_b, 0, P)
-        scatter(q_tok1, q_sb0a[1][:], list_b, 0, P)
-        dc_q1 = (tile("dc1_codes", [P, C], U32, "q_sb0a0"), tile("dc1_codes_sc", [P, C], U8))
-        for u in range(2):
-            cols = slice(u * P, (u + 1) * P)
-            nc.vector.quantize_mx(out=dc_q1[0][:, cols].bitcast(FP8X4), scales=dc_q1[1][:, cols], in_=dc_slots1[u][:])
-        scatter(q_tok0, q_sb0b[:, 0, :], list_b, P, P)
-        scatter(q_tok1, q_sb0b[:, 1, :], list_b, P, P)
-        q_sb1 = [tile(f"q_sb1{kh}", [P, C], F32) for kh in range(2)]
-        for kh in range(2):
-            q_ps1 = ps.tile([P, C], F32, name=f"q_ps1{kh}", tag=f"r_ps1{kh}")
-            expert_product(q_ps1[:], wb, wb_sc, 1, kh, dc_q1)
-            leave_psum(q_sb1[kh][:], q_ps1[:])
-        scatter(q_tok0, q_sb1[0][:], list_b, C, C)
+        scatter_v(q_tok[0], leave_psum_v("q_sb00", q_ps[0, 0]), list_b, 0)
+        scatter_s(q_tok[1], leave_psum_s("q_sb01", q_ps[0, 1]), list_b, 0)
+        q_sb10 = leave_psum_v("q_sb10", q_ps[1, 0])
+        r_sb11 = leave_psum_v("r_sb11", r_ps[1, 1], "q_sb00")
+        scatter_v(q_tok[0], q_sb10, list_b, 1)
         total = [tile(f"total{kh}", [P, T], F32) for kh in range(2)]
-        nc.gpsimd.tensor_tensor(out=total[0][:], in0=r_tok[0][:], in1=q_tok0[:], op=ADD)
+        nc.gpsimd.tensor_tensor(out=total[0][:], in0=r_tok[0][:], in1=q_tok[0][:], op=ADD)
         nc.sync.dma_start(out=out[0:P, :], in_=total[0][:])
-        scatter(q_tok1, q_sb1[1][:], list_b, C, C)
+        scatter_s(q_tok[1], leave_psum_s("q_sb11", q_ps[1, 1]), list_b, 1)
+        scatter_v(r_tok[1], r_sb11, list_a, 1)
         for th in range(2):
-            nc.vector.tensor_tensor(out=total[1][:, halves[th]], in0=r_tok[1][:, halves[th]], in1=q_tok1[:, halves[th]], op=ADD)
+            nc.vector.tensor_tensor(out=total[1][:, halves[th]], in0=r_tok[1][:, halves[th]], in1=q_tok[1][:, halves[th]], op=ADD)
             (nc.scalar if th == 0 else nc.sync).dma_start(out=out[P:2 * P, halves[th]], in_=total[1][:, halves[th]])

@@ -85,10 +85,9 @@ def tile_moe_plb_none_kernel(
         for key in parts:
             load_part(c_sb, c, key)
         nc.sync.dma_start(list_a[:], offs)
-        for key in parts[:2]:
-            load_part(a_sb, a, key)
+        load_part(a_sb, a, parts[0])
         load_expert(wa, wa_sc, wat_words, wat_scales)
-        for key in parts[2:]:
+        for key in (parts[1], parts[3], parts[2]):
             load_part(a_sb, a, key)
         nc.sync.dma_start(list_b[:], offs2)
         load_expert(wb, wb_sc, wbt_words, wbt_scales)
@@ -119,14 +118,14 @@ def tile_moe_plb_none_kernel(
             return lst[:, first // 16:(first + count) // 16]
 
         def gather_pairs(slots, h, pairs, lst, first, count):
-            words = slots[:].bitcast(U32).rearrange("p (s h) -> p s h", h=2)
-            window = pairs[:].rearrange("p t j -> p (t j)").bitcast(U32)
+            words = slots.bitcast(U32).rearrange("p (s h) -> p s h", h=2)
+            window = pairs.rearrange("p t j -> p (t j)").bitcast(U32)
             nc.vector.tensor_copy(out=words[:, :, h], in_=window.indirect(slots_of(lst, first, count)))
 
         def quantize(name, slots, width, tag=None):
             codes = tile(f"{name}_codes", [P, width], U32, tag)
             codes_sc = tile(f"{name}_codes_sc", [P, width], U8)
-            nc.vector.quantize_mx(out=codes[:].bitcast(FP8X4), scales=codes_sc[:], in_=slots[:])
+            nc.vector.quantize_mx(out=codes[:].bitcast(FP8X4), scales=codes_sc[:], in_=slots)
             return codes, codes_sc
 
         def expert_product(dst, words, scales, e, kh, quantized):
@@ -155,8 +154,10 @@ def tile_moe_plb_none_kernel(
         def scatter_s(tok, res, lst, e):
             nc.scalar.activation(out=tok[:].indirect(slots_of(lst, e * C, C)), in_=res[:], func=COPY)
 
-        da = [tile(f"da{h}", [P, T, 2], BF16) for h in range(2)]
-        dc = [tile(f"dc{h}", [P, T, 2], BF16) for h in range(2)]
+        da = [tile(f"da{h}", [P, T, 2], BF16)[:] for h in range(2)]
+        shared = tile("shared", [P, 5 * T], BF16)
+        dc = [shared[:, first:first + 2 * T].rearrange("p (t j) -> p t j", j=2) for first in (0, 3 * T)]
+        da_slots = [shared[:, first:first + 4 * C] for first in (T, 2 * T)]
 
         def product_v(dst, saved, h, th):
             nc.vector.tensor_tensor(
@@ -168,17 +169,26 @@ def tile_moe_plb_none_kernel(
 
         for h, th in parts:
             product_v(da, c_sb, h, th)
+        dh_copy = {}
         for h, th in parts[:3]:
             dh_sb = tile(f"dh_sb{h}{th}", [P, HALF, 2], F32)
             nc.scalar.copy(out=dh_sb[:], in_=dh[h, th][:].rearrange("p j t -> p t j"))
-            nc.gpsimd.tensor_tensor(out=dc[h][:, halves[th], :], in0=dh_sb[:], in1=a_sb[h, th][:].rearrange("p j t -> p t j"), op=MULT)
+            dh_copy[h, th] = dh_sb
+
+        def product_g(h, th):
+            nc.gpsimd.tensor_tensor(out=dc[h][:, halves[th], :], in0=dh_copy[h, th][:], in1=a_sb[h, th][:].rearrange("p j t -> p t j"), op=MULT)
+
+        product_g(*parts[0])
 
         r_ps = {}
         for e in range(E):
-            slots = tile(f"da_slots{e}", [P, 4 * C], BF16)
+            slots = da_slots[e]
             for h in range(2):
                 gather_pairs(slots, h, da[h], list_a, e * C, C)
             quantized = quantize(f"da_q{e}", slots, C)
+            product_g(*parts[1 + e])
+            if e == 0:
+                product_v(dc, a_sb, *parts[3])
             for kh in range(2):
                 r_ps[e, kh] = bank(f"r_ps{e}{kh}", [P, C])
                 expert_product(r_ps[e, kh][:], wa, wa_sc, e, kh, quantized)
@@ -186,11 +196,10 @@ def tile_moe_plb_none_kernel(
         r_tok = [tile(f"r_tok{kh}", [P, T], F32) for kh in range(2)]
         q_tok = [tile(f"q_tok{kh}", [P, T], F32) for kh in range(2)]
         scatter_s(r_tok[0], leave_psum_s("r_sb00", r_ps[0, 0]), list_a, 0)
-        scatter_s(r_tok[0], leave_psum_s("r_sb10", r_ps[1, 0]), list_a, 1)
         scatter_s(r_tok[1], leave_psum_s("r_sb01", r_ps[0, 1]), list_a, 0)
+        scatter_s(r_tok[0], leave_psum_s("r_sb10", r_ps[1, 0]), list_a, 1)
 
-        product_v(dc, a_sb, *parts[3])
-        dc_slots = [tile(f"dc_slots{e}", [P, 4 * C], BF16) for e in range(E)]
+        dc_slots = [tile(f"dc_slots{e}", [P, 4 * C], BF16)[:] for e in range(E)]
         for e in range(E):
             gather_pairs(dc_slots[e], 0, dc[0], list_b, e * C, C)
         q_ps = {}
@@ -202,9 +211,10 @@ def tile_moe_plb_none_kernel(
                 expert_product(q_ps[e, kh][:], wb, wb_sc, e, kh, quantized)
 
         scatter_v(q_tok[0], leave_psum_v("q_sb00", q_ps[0, 0]), list_b, 0)
-        scatter_s(q_tok[1], leave_psum_s("q_sb01", q_ps[0, 1]), list_b, 0)
-        q_sb10 = leave_psum_v("q_sb10", q_ps[1, 0])
-        r_sb11 = leave_psum_v("r_sb11", r_ps[1, 1], "q_sb00")
+        q_sb10 = leave_psum_s("q_sb10", q_ps[1, 0])
+        q_sb01 = leave_psum_s("q_sb01", q_ps[0, 1], "dc_q1_codes")
+        r_sb11 = leave_psum_s("r_sb11", r_ps[1, 1], "dc_q1_codes_sc")
+        scatter_s(q_tok[1], q_sb01, list_b, 0)
         scatter_v(q_tok[0], q_sb10, list_b, 1)
         total = [tile(f"total{kh}", [P, T], F32) for kh in range(2)]
         nc.gpsimd.tensor_tensor(out=total[0][:], in0=r_tok[0][:], in1=q_tok[0][:], op=ADD)

@@ -138,21 +138,21 @@ def tile_moe_plb_none_kernel(
                 start=True, stop=True,
             )
 
-        def leave_psum_s(name, src, tag=None):
-            dst = tile(name, [P, C], F32, tag)
-            nc.scalar.copy(out=dst[:], in_=src[:])
+        def leave_psum_s(name, src, tag=None, first=0, count=C):
+            dst = tile(name, [P, count], F32, tag)
+            nc.scalar.copy(out=dst[:], in_=src[:, first:first + count])
             return dst
 
-        def leave_psum_v(name, src, tag=None):
-            dst = tile(name, [P, C], F32, tag)
-            nc.vector.tensor_copy(out=dst[:], in_=src[:])
+        def leave_psum_v(name, src, tag=None, first=0, count=C):
+            dst = tile(name, [P, count], F32, tag)
+            nc.vector.tensor_copy(out=dst[:], in_=src[:, first:first + count])
             return dst
 
-        def scatter_v(tok, res, lst, e):
-            nc.vector.tensor_copy(out=tok[:].indirect(slots_of(lst, e * C, C)), in_=res[:])
+        def scatter_v(tok, res, lst, first, count=C):
+            nc.vector.tensor_copy(out=tok[:].indirect(slots_of(lst, first, count)), in_=res[:])
 
-        def scatter_s(tok, res, lst, e):
-            nc.scalar.activation(out=tok[:].indirect(slots_of(lst, e * C, C)), in_=res[:], func=COPY)
+        def scatter_s(tok, res, lst, first, count=C):
+            nc.scalar.activation(out=tok[:].indirect(slots_of(lst, first, count)), in_=res[:], func=COPY)
 
         da = [tile(f"da{h}", [P, T, 2], BF16)[:] for h in range(2)]
         shared = tile("shared", [P, 5 * T], BF16)
@@ -197,7 +197,8 @@ def tile_moe_plb_none_kernel(
         q_tok = [tile(f"q_tok{kh}", [P, T], F32) for kh in range(2)]
         scatter_s(r_tok[0], leave_psum_s("r_sb00", r_ps[0, 0]), list_a, 0)
         scatter_s(r_tok[1], leave_psum_s("r_sb01", r_ps[0, 1]), list_a, 0)
-        scatter_s(r_tok[0], leave_psum_s("r_sb10", r_ps[1, 0]), list_a, 1)
+        scatter_s(r_tok[0], leave_psum_s("r_sb10", r_ps[1, 0]), list_a, C)
+        scatter_s(r_tok[1], leave_psum_s("r_sb11a", r_ps[1, 1], None, 0, P), list_a, C, P)
 
         dc_slots = [tile(f"dc_slots{e}", [P, 4 * C], BF16)[:] for e in range(E)]
         for e in range(E):
@@ -213,14 +214,14 @@ def tile_moe_plb_none_kernel(
         scatter_v(q_tok[0], leave_psum_v("q_sb00", q_ps[0, 0]), list_b, 0)
         q_sb10 = leave_psum_s("q_sb10", q_ps[1, 0])
         q_sb01 = leave_psum_s("q_sb01", q_ps[0, 1], "dc_q1_codes")
-        r_sb11 = leave_psum_s("r_sb11", r_ps[1, 1], "dc_q1_codes_sc")
+        r_sb11 = leave_psum_v("r_sb11b", r_ps[1, 1], "q_sb00", P, P)
         scatter_s(q_tok[1], q_sb01, list_b, 0)
-        scatter_v(q_tok[0], q_sb10, list_b, 1)
+        scatter_v(q_tok[0], q_sb10, list_b, C)
         total = [tile(f"total{kh}", [P, T], F32) for kh in range(2)]
         nc.gpsimd.tensor_tensor(out=total[0][:], in0=r_tok[0][:], in1=q_tok[0][:], op=ADD)
         nc.sync.dma_start(out=out[0:P, :], in_=total[0][:])
-        scatter_s(q_tok[1], leave_psum_s("q_sb11", q_ps[1, 1]), list_b, 1)
-        scatter_v(r_tok[1], r_sb11, list_a, 1)
+        scatter_s(q_tok[1], leave_psum_s("q_sb11", q_ps[1, 1]), list_b, C)
+        scatter_v(r_tok[1], r_sb11, list_a, C + P, P)
         for th in range(2):
             nc.vector.tensor_tensor(out=total[1][:, halves[th]], in0=r_tok[1][:, halves[th]], in1=q_tok[1][:, halves[th]], op=ADD)
             (nc.scalar if th == 0 else nc.sync).dma_start(out=out[P:2 * P, halves[th]], in_=total[1][:, halves[th]])

@@ -48,7 +48,7 @@ def tile_moe_plb_none_kernel(
         wa_sc = tile("wa_sc", [P, E, K], U8)
         wb_sc = tile("wb_sc", [P, E, K], U8)
         halves = [slice(0, HALF), slice(HALF, T)]
-        parts = [(h, th) for h in range(2) for th in range(2)]
+        parts = [(h, th) for h in (1, 0) for th in range(2)]
         c_sb = {k: tile(f"c{k[0]}{k[1]}", [P, 2, HALF], F32) for k in parts}
         a_sb = {k: tile(f"a{k[0]}{k[1]}", [P, 2, HALF], F32) for k in parts}
 
@@ -82,21 +82,23 @@ def tile_moe_plb_none_kernel(
         nc.sync.dma_start(out=dy[:].bitcast(I32), in_=dy_words[0].rearrange("p t d -> p (t d)").bitcast(I32))
         for q in range(2, 4):
             load_scales(dy_sc, dy_scales, q)
-        for key in parts:
+        for key in parts[:2]:
             load_part(c_sb, c, key)
         nc.sync.dma_start(list_a[:], offs)
+        load_part(c_sb, c, parts[2])
         load_part(a_sb, a, parts[0])
-        load_expert(wa, wa_sc, wat_words, wat_scales)
-        for key in (parts[1], parts[3], parts[2]):
+        load_part(c_sb, c, parts[3])
+        for key in (parts[2], parts[1], parts[3]):
             load_part(a_sb, a, key)
         nc.sync.dma_start(list_b[:], offs2)
+        load_expert(wa, wa_sc, wat_words, wat_scales)
         load_expert(wb, wb_sc, wbt_words, wbt_scales)
 
         w2_in = w2_raw[:].bitcast(U16).rearrange("p (m j) -> p j m", j=4)
         w2_out = w2[:].bitcast(U16).rearrange("p (j m) -> p j m", j=4)
         sc_in = w2_sc_raw[:].rearrange("p (m j) -> p j m", j=4)
         sc_out = w2_sc[:].rearrange("p (j m) -> p j m", j=4)
-        for js in (slice(0, 2), slice(2, 4)):
+        for js in (slice(2, 4), slice(0, 2)):
             nc.vector.tensor_copy(out=sc_out[:, js, :], in_=sc_in[:, js, :])
             nc.vector.tensor_copy(out=w2_out[:, js, :], in_=w2_in[:, js, :])
 
@@ -154,74 +156,86 @@ def tile_moe_plb_none_kernel(
         def scatter_s(tok, res, lst, first, count=C):
             nc.scalar.activation(out=tok[:].indirect(slots_of(lst, first, count)), in_=res[:], func=COPY)
 
-        da = [tile(f"da{h}", [P, T, 2], BF16)[:] for h in range(2)]
-        shared = tile("shared", [P, 5 * T], BF16)
-        dc = [shared[:, first:first + 2 * T].rearrange("p (t j) -> p t j", j=2) for first in (0, 3 * T)]
-        da_slots = [shared[:, first:first + 4 * C] for first in (T, 2 * T)]
+        da_lo = tile("da_lo", [P, T, 2], BF16)[:]
+        da_hi = tile("da_hi", [P, 2, T], BF16)
+        dc = [tile(f"dc{h}", [P, T, 2], BF16)[:] for h in range(2)]
+        shared = tile("shared", [P, 4 * C], F32)
+        da_slots = [shared[:, 2 * C:4 * C].bitcast(BF16), tile("da_slots1", [P, 4 * C], BF16)[:]]
+        dh_copy = [shared[:, 1:2 * C + 1].rearrange("p (t j) -> p t j", j=2), tile("dh_sb1", [P, HALF, 2], F32)[:]]
 
-        def product_v(dst, saved, h, th):
+        def product_v(dst, saved, th):
             nc.vector.tensor_tensor(
-                out=dst[h][:, halves[th], :].rearrange("p (g i) j -> p g j i", i=4),
-                in0=dh[h, th][:].rearrange("p j (g i) -> p g j i", i=4),
-                in1=saved[h, th][:].rearrange("p j (g i) -> p g j i", i=4),
+                out=dst[:, halves[th], :].rearrange("p (g i) j -> p g j i", i=4),
+                in0=dh[0, th][:].rearrange("p j (g i) -> p g j i", i=4),
+                in1=saved[0, th][:].rearrange("p j (g i) -> p g j i", i=4),
                 op=MULT,
             )
 
-        for h, th in parts:
-            product_v(da, c_sb, h, th)
-        dh_copy = {}
-        for h, th in parts[:3]:
-            dh_sb = tile(f"dh_sb{h}{th}", [P, HALF, 2], F32)
-            nc.scalar.copy(out=dh_sb[:], in_=dh[h, th][:].rearrange("p j t -> p t j"))
-            dh_copy[h, th] = dh_sb
+        def product_g(th):
+            nc.scalar.copy(out=dh_copy[th], in_=dh[1, th][:].rearrange("p j t -> p t j"))
+            nc.gpsimd.tensor_tensor(out=dc[1][:, halves[th], :], in0=dh_copy[th], in1=a_sb[1, th][:].rearrange("p j t -> p t j"), op=MULT)
 
-        def product_g(h, th):
-            nc.gpsimd.tensor_tensor(out=dc[h][:, halves[th], :], in0=dh_copy[h, th][:], in1=a_sb[h, th][:].rearrange("p j t -> p t j"), op=MULT)
+        def gather_plane(slots, i, e):
+            nc.scalar.activation(out=slots.rearrange("p (s j) -> p s j", j=4)[:, :, 2 + i], in_=da_hi[:, i, :].indirect(slots_of(list_a, e * C, C)), func=COPY)
 
-        product_g(*parts[0])
+        for th in range(2):
+            nc.vector.tensor_tensor(out=da_hi[:, :, halves[th]], in0=dh[1, th][:], in1=c_sb[1, th][:], op=MULT)
+        for th in range(2):
+            product_v(da_lo, c_sb, th)
+        product_g(0)
+        gather_plane(da_slots[0], 0, 0)
+        product_g(1)
+        gather_plane(da_slots[0], 1, 0)
+        product_v(dc[0], a_sb, 0)
+        for e in (1, 0):
+            gather_pairs(da_slots[e], 0, da_lo, list_a, e * C, C)
+        product_v(dc[0], a_sb, 1)
+        for i in range(2):
+            gather_plane(da_slots[1], i, 1)
 
-        r_ps = {}
-        for e in range(E):
-            slots = da_slots[e]
-            for h in range(2):
-                gather_pairs(slots, h, da[h], list_a, e * C, C)
-            quantized = quantize(f"da_q{e}", slots, C)
-            product_g(*parts[1 + e])
-            if e == 0:
-                product_v(dc, a_sb, *parts[3])
+        dc_slots = [tile(f"dc_slots{e}", [P, 4 * C], BF16)[:] for e in range(E)]
+        r_ps, q_ps = {}, {}
+
+        def expert_a(e, tag):
+            quantized = quantize(f"da_q{e}", da_slots[e], C, tag)
             for kh in range(2):
                 r_ps[e, kh] = bank(f"r_ps{e}{kh}", [P, C])
                 expert_product(r_ps[e, kh][:], wa, wa_sc, e, kh, quantized)
 
-        r_tok = [tile(f"r_tok{kh}", [P, T], F32) for kh in range(2)]
-        q_tok = [tile(f"q_tok{kh}", [P, T], F32) for kh in range(2)]
-        scatter_s(r_tok[0], leave_psum_s("r_sb00", r_ps[0, 0]), list_a, 0)
-        scatter_s(r_tok[1], leave_psum_s("r_sb01", r_ps[0, 1]), list_a, 0)
-        scatter_s(r_tok[0], leave_psum_s("r_sb10", r_ps[1, 0]), list_a, C)
-        scatter_s(r_tok[1], leave_psum_s("r_sb11a", r_ps[1, 1], None, 0, P), list_a, C, P)
-
-        dc_slots = [tile(f"dc_slots{e}", [P, 4 * C], BF16)[:] for e in range(E)]
-        for e in range(E):
-            gather_pairs(dc_slots[e], 0, dc[0], list_b, e * C, C)
-        q_ps = {}
-        for e in range(E):
-            gather_pairs(dc_slots[e], 1, dc[1], list_b, e * C, C)
+        def expert_b(e):
             quantized = quantize(f"dc_q{e}", dc_slots[e], C)
             for kh in range(2):
                 q_ps[e, kh] = bank(f"q_ps{e}{kh}", [P, C], f"dh{e}{kh}")
                 expert_product(q_ps[e, kh][:], wb, wb_sc, e, kh, quantized)
 
-        scatter_v(q_tok[0], leave_psum_v("q_sb00", q_ps[0, 0]), list_b, 0)
-        q_sb10 = leave_psum_s("q_sb10", q_ps[1, 0])
-        q_sb01 = leave_psum_s("q_sb01", q_ps[0, 1], "dc_q1_codes")
-        r_sb11 = leave_psum_v("r_sb11b", r_ps[1, 1], "q_sb00", P, P)
+        expert_a(0, "dh_sb1")
+        gather_pairs(dc_slots[0], 1, dc[1], list_b, 0, C)
+        expert_a(1, "a11")
+        gather_pairs(dc_slots[0], 0, dc[0], list_b, 0, C)
+        gather_pairs(dc_slots[1], 1, dc[1], list_b, C, C)
+        expert_b(0)
+        gather_pairs(dc_slots[1], 0, dc[0], list_b, C, C)
+
+        r_tok = [tile(f"r_tok{kh}", [P, T], F32) for kh in range(2)]
+        q_tok = [tile(f"q_tok{kh}", [P, T], F32) for kh in range(2)]
+        scatter_s(r_tok[0], leave_psum_s("r_sb00", r_ps[0, 0]), list_a, 0)
+        scatter_s(r_tok[1], leave_psum_s("r_sb01", r_ps[0, 1]), list_a, 0)
+        scatter_s(r_tok[0], leave_psum_v("r_sb10", r_ps[1, 0], "dc_slots0"), list_a, C)
+
+        q_sb00 = leave_psum_v("q_sb00", q_ps[0, 0])
+        expert_b(1)
+        q_sb01 = leave_psum_v("q_sb01", q_ps[0, 1])
+        scatter_v(q_tok[0], q_sb00, list_b, 0)
         scatter_s(q_tok[1], q_sb01, list_b, 0)
+        q_sb10 = leave_psum_v("q_sb10", q_ps[1, 0])
+        q_sb11 = leave_psum_v("q_sb11", q_ps[1, 1])
+        r_sb11 = leave_psum_v("r_sb11", r_ps[1, 1], "q_sb00")
         scatter_v(q_tok[0], q_sb10, list_b, C)
         total = [tile(f"total{kh}", [P, T], F32) for kh in range(2)]
         nc.gpsimd.tensor_tensor(out=total[0][:], in0=r_tok[0][:], in1=q_tok[0][:], op=ADD)
         nc.sync.dma_start(out=out[0:P, :], in_=total[0][:])
-        scatter_s(q_tok[1], leave_psum_s("q_sb11", q_ps[1, 1]), list_b, C)
-        scatter_v(r_tok[1], r_sb11, list_a, C + P, P)
+        scatter_s(q_tok[1], q_sb11, list_b, C)
+        scatter_v(r_tok[1], r_sb11, list_a, C)
         for th in range(2):
             nc.vector.tensor_tensor(out=total[1][:, halves[th]], in0=r_tok[1][:, halves[th]], in1=q_tok[1][:, halves[th]], op=ADD)
             (nc.scalar if th == 0 else nc.sync).dma_start(out=out[P:2 * P, halves[th]], in_=total[1][:, halves[th]])

@@ -19,6 +19,7 @@ ADD = mybir.AluOpType.add
 COPY = mybir.ActivationFunctionType.Copy
 P = 128
 HALF = 256
+FIRST = 128
 
 
 def tile_moe_plb_none_kernel(
@@ -88,7 +89,7 @@ def tile_moe_plb_none_kernel(
         load_part(c_sb, c, parts[2])
         load_part(a_sb, a, parts[0])
         load_part(c_sb, c, parts[3])
-        for key in (parts[2], parts[1], parts[3]):
+        for key in (parts[3], parts[1], parts[2]):
             load_part(a_sb, a, key)
         nc.sync.dma_start(list_b[:], offs2)
         load_expert(wa, wa_sc, wat_words, wat_scales)
@@ -124,9 +125,9 @@ def tile_moe_plb_none_kernel(
             window = pairs.rearrange("p t j -> p (t j)").bitcast(U32)
             nc.vector.tensor_copy(out=words[:, :, h], in_=window.indirect(slots_of(lst, first, count)))
 
-        def quantize(name, slots, width, tag=None):
+        def quantize(name, slots, width, tag=None, sc_tag=None):
             codes = tile(f"{name}_codes", [P, width], U32, tag)
-            codes_sc = tile(f"{name}_codes_sc", [P, width], U8)
+            codes_sc = tile(f"{name}_codes_sc", [P, width], U8, sc_tag)
             nc.vector.quantize_mx(out=codes[:].bitcast(FP8X4), scales=codes_sc[:], in_=slots)
             return codes, codes_sc
 
@@ -158,16 +159,16 @@ def tile_moe_plb_none_kernel(
 
         da_lo = tile("da_lo", [P, T, 2], BF16)[:]
         da_hi = tile("da_hi", [P, 2, T], BF16)
-        dc = [tile(f"dc{h}", [P, T, 2], BF16)[:] for h in range(2)]
-        shared = tile("shared", [P, 4 * C], F32)
+        shared = tile("shared", [P, 6 * C], F32)
+        dc = [shared[:, 4 * C - 16:6 * C - 16].bitcast(BF16).rearrange("p (t j) -> p t j", j=2), tile("dc1", [P, T, 2], BF16)[:]]
         da_slots = [shared[:, 2 * C:4 * C].bitcast(BF16), tile("da_slots1", [P, 4 * C], BF16)[:]]
         dh_copy = [shared[:, 1:2 * C + 1].rearrange("p (t j) -> p t j", j=2), tile("dh_sb1", [P, HALF, 2], F32)[:]]
 
-        def product_v(dst, saved, th):
+        def product_v(dst, saved, th, first=0):
             nc.vector.tensor_tensor(
-                out=dst[:, halves[th], :].rearrange("p (g i) j -> p g j i", i=4),
-                in0=dh[0, th][:].rearrange("p j (g i) -> p g j i", i=4),
-                in1=saved[0, th][:].rearrange("p j (g i) -> p g j i", i=4),
+                out=dst[:, HALF * th + first:HALF * (th + 1), :].rearrange("p (g i) j -> p g j i", i=4),
+                in0=dh[0, th][:, :, first:].rearrange("p j (g i) -> p g j i", i=4),
+                in1=saved[0, th][:, :, first:].rearrange("p j (g i) -> p g j i", i=4),
                 op=MULT,
             )
 
@@ -186,33 +187,36 @@ def tile_moe_plb_none_kernel(
         gather_plane(da_slots[0], 0, 0)
         product_g(1)
         gather_plane(da_slots[0], 1, 0)
-        product_v(dc[0], a_sb, 0)
+        dh_first = tile("dh_first", [P, FIRST, 2], F32)
+        nc.scalar.copy(out=dh_first[:], in_=dh[0, 0][:, :, :FIRST].rearrange("p j t -> p t j"))
+        product_v(dc[0], a_sb, 1)
         for e in (1, 0):
             gather_pairs(da_slots[e], 0, da_lo, list_a, e * C, C)
-        product_v(dc[0], a_sb, 1)
+        product_v(dc[0], a_sb, 0, FIRST)
         for i in range(2):
             gather_plane(da_slots[1], i, 1)
 
         dc_slots = [tile(f"dc_slots{e}", [P, 4 * C], BF16)[:] for e in range(E)]
         r_ps, q_ps = {}, {}
 
-        def expert_a(e, tag):
-            quantized = quantize(f"da_q{e}", da_slots[e], C, tag)
+        def expert_a(e, tag, sc_tag=None):
+            quantized = quantize(f"da_q{e}", da_slots[e], C, tag, sc_tag)
             for kh in range(2):
                 r_ps[e, kh] = bank(f"r_ps{e}{kh}", [P, C])
                 expert_product(r_ps[e, kh][:], wa, wa_sc, e, kh, quantized)
 
         def expert_b(e):
-            quantized = quantize(f"dc_q{e}", dc_slots[e], C)
+            quantized = quantize(f"dc_q{e}", dc_slots[e], C, "dc_codes")
             for kh in range(2):
                 q_ps[e, kh] = bank(f"q_ps{e}{kh}", [P, C], f"dh{e}{kh}")
                 expert_product(q_ps[e, kh][:], wb, wb_sc, e, kh, quantized)
 
         expert_a(0, "dh_sb1")
-        gather_pairs(dc_slots[0], 1, dc[1], list_b, 0, C)
-        expert_a(1, "a11")
+        nc.gpsimd.tensor_tensor(out=dc[0][:, :FIRST, :], in0=dh_first[:], in1=a_sb[0, 0][:, :, :FIRST].rearrange("p j t -> p t j"), op=MULT)
+        for e in range(E):
+            gather_pairs(dc_slots[e], 1, dc[1], list_b, e * C, C)
         gather_pairs(dc_slots[0], 0, dc[0], list_b, 0, C)
-        gather_pairs(dc_slots[1], 1, dc[1], list_b, C, C)
+        expert_a(1, "dc1", "dh_first")
         expert_b(0)
         gather_pairs(dc_slots[1], 0, dc[0], list_b, C, C)
 

from contextlib import ExitStack

import concourse.mybir as mybir

K, T, H, N = 256, 512, 512, 512
E, C = 2, 256
FLOPS = 2 * N * H * T + 2 * 2 * H * K * T

F32 = mybir.dt.float32
BF16 = mybir.dt.bfloat16
I32 = mybir.dt.int32
U32 = mybir.dt.uint32
U16 = mybir.dt.uint16
U8 = mybir.dt.uint8
FP8X4 = mybir.dt.float8_e4m3fn_x4
FP4X4 = mybir.dt.float4_e2m1fn_x4
MULT = mybir.AluOpType.mult
ADD = mybir.AluOpType.add
COPY = mybir.ActivationFunctionType.Copy
P = 128
HALF = 256
FIRST = 128


def tile_moe_plb_none_kernel(
    tc, dy_words, dy_scales, w2t_words, w2t_scales, wat_words, wat_scales, wbt_words, wbt_scales, a, c, offs, offs2, out
):
    nc = tc.nc
    with ExitStack() as ctx:
        sb = ctx.enter_context(tc.tile_pool(name="sb", bufs=1))
        ps = ctx.enter_context(tc.psum_pool(name="ps", bufs=1))

        def tile(name, shape, dtype, tag=None):
            return sb.tile(shape, dtype, name=name, tag=tag or name, align_bytes=64)

        def bank(name, shape, tag=None):
            return ps.tile(shape, F32, name=name, tag=tag or name)

        list_a = tile("list_a", [P, T // 16], U16)
        list_b = tile("list_b", [P, T // 16], U16)
        w2_raw = tile("w2_raw", [P, 2 * H], U8)
        w2_sc_raw = tile("w2_sc_raw", [P, H], U8)
        w2 = tile("w2", [P, 2 * H], U8)
        w2_sc = tile("w2_sc", [P, H], U8)
        dy = tile("dy", [P, T], U32)
        dy_sc = tile("dy_sc", [P, T], U8)
        wa = tile("wa", [P, E, 2 * K], U8)
        wb = tile("wb", [P, E, 2 * K], U8)
        wa_sc = tile("wa_sc", [P, E, K], U8)
        wb_sc = tile("wb_sc", [P, E, K], U8)
        halves = [slice(0, HALF), slice(HALF, T)]
        parts = [(h, th) for h in (1, 0) for th in range(2)]
        c_sb = {k: tile(f"c{k[0]}{k[1]}", [P, 2, HALF], F32) for k in parts}
        a_sb = {k: tile(f"a{k[0]}{k[1]}", [P, 2, HALF], F32) for k in parts}

        nc.vector.memset(w2_sc_raw[:].bitcast(I32), 0)
        warm = tile("warm", [P, 2], F32)
        nc.vector.memset(warm[:, 0:1], 0.0)
        nc.scalar.activation(out=warm[:, 1:2], in_=warm[:, 0:1], func=COPY)

        def rows(q):
            return slice(32 * q, 32 * q + 4), slice(4 * q, 4 * q + 4)

        def load_scales(dst, src, q):
            part, row = rows(q)
            nc.sync.dma_start(out=dst[part, :].bitcast(I32), in_=src[0, row, :].bitcast(I32))

        def load_expert(words, scales, w_src, s_src):
            nc.sync.dma_start(out=words[:].bitcast(I32), in_=w_src[:, 0].rearrange("e p n -> p e n").bitcast(I32))
            for q in range(4):
                part, row = rows(q)
                nc.sync.dma_start(out=scales[part].bitcast(I32), in_=s_src[:, 0, row, :].rearrange("e r n -> r e n").bitcast(I32))

        def load_part(dst, src, key):
            h, th = key
            nc.sync.dma_start(out=dst[key][:], in_=src.rearrange("(p j) t -> p j t", j=4)[:, 2 * h:2 * h + 2, halves[th]])

        for q in range(2):
            load_scales(dy_sc, dy_scales, q)
        nc.sync.dma_start(out=w2_raw[:].bitcast(I32), in_=w2t_words[0].bitcast(I32))
        for q in range(4):
            load_scales(w2_sc_raw, w2t_scales, q)
        nc.sync.dma_start(out=dy[:].bitcast(I32), in_=dy_words[0].rearrange("p t d -> p (t d)").bitcast(I32))
        for q in range(2, 4):
            load_scales(dy_sc, dy_scales, q)
        for key in parts[:2]:
            load_part(c_sb, c, key)
        nc.sync.dma_start(list_a[:], offs)
        load_part(c_sb, c, parts[2])
        load_part(a_sb, a, parts[0])
        load_part(c_sb, c, parts[3])
        for key in (parts[3], parts[1], parts[2]):
            load_part(a_sb, a, key)
        nc.sync.dma_start(list_b[:], offs2)
        load_expert(wa, wa_sc, wat_words, wat_scales)
        load_expert(wb, wb_sc, wbt_words, wbt_scales)

        w2_in = w2_raw[:].bitcast(U16).rearrange("p (m j) -> p j m", j=4)
        w2_out = w2[:].bitcast(U16).rearrange("p (j m) -> p j m", j=4)
        sc_in = w2_sc_raw[:].rearrange("p (m j) -> p j m", j=4)
        sc_out = w2_sc[:].rearrange("p (j m) -> p j m", j=4)
        for js in (slice(2, 4), slice(0, 2)):
            nc.vector.tensor_copy(out=sc_out[:, js, :], in_=sc_in[:, js, :])
            nc.vector.tensor_copy(out=w2_out[:, js, :], in_=w2_in[:, js, :])

        dh = {}
        for h, th in parts:
            dh[h, th] = bank(f"dh{h}{th}", [P, 2, HALF])
            for i in range(2):
                j = 2 * h + i
                nc.tensor.matmul_mx(
                    out=dh[h, th][:, i, :],
                    lhsT=w2[:, 2 * P * j:2 * P * (j + 1)].bitcast(FP4X4),
                    lhsT_scale=w2_sc[:, P * j:P * (j + 1)],
                    rhs=dy[:, halves[th]].bitcast(FP8X4),
                    rhs_scale=dy_sc[:, halves[th]],
                    start=True, stop=True,
                )

        def slots_of(lst, first, count):
            return lst[:, first // 16:(first + count) // 16]

        def gather_pairs(slots, h, pairs, lst, first, count):
            words = slots.bitcast(U32).rearrange("p (s h) -> p s h", h=2)
            window = pairs.rearrange("p t j -> p (t j)").bitcast(U32)
            nc.vector.tensor_copy(out=words[:, :, h], in_=window.indirect(slots_of(lst, first, count)))

        def quantize(name, slots, width, tag=None, sc_tag=None):
            codes = tile(f"{name}_codes", [P, width], U32, tag)
            codes_sc = tile(f"{name}_codes_sc", [P, width], U8, sc_tag)
            nc.vector.quantize_mx(out=codes[:].bitcast(FP8X4), scales=codes_sc[:], in_=slots)
            return codes, codes_sc

        def expert_product(dst, words, scales, e, kh, quantized):
            nc.tensor.matmul_mx(
                out=dst,
                lhsT=words[:, e, 2 * P * kh:2 * P * (kh + 1)].bitcast(FP4X4),
                lhsT_scale=scales[:, e, P * kh:P * (kh + 1)],
                rhs=quantized[0][:].bitcast(FP8X4),
                rhs_scale=quantized[1][:],
                start=True, stop=True,
            )

        def leave_psum_s(name, src, tag=None, first=0, count=C):
            dst = tile(name, [P, count], F32, tag)
            nc.scalar.copy(out=dst[:], in_=src[:, first:first + count])
            return dst

        def leave_psum_v(name, src, tag=None, first=0, count=C):
            dst = tile(name, [P, count], F32, tag)
            nc.vector.tensor_copy(out=dst[:], in_=src[:, first:first + count])
            return dst

        def scatter_v(tok, res, lst, first, count=C):
            nc.vector.tensor_copy(out=tok[:].indirect(slots_of(lst, first, count)), in_=res[:])

        def scatter_s(tok, res, lst, first, count=C):
            nc.scalar.activation(out=tok[:].indirect(slots_of(lst, first, count)), in_=res[:], func=COPY)

        da_lo = tile("da_lo", [P, T, 2], BF16)[:]
        da_hi = tile("da_hi", [P, 2, T], BF16)
        shared = tile("shared", [P, 6 * C], F32)
        dc = [shared[:, 4 * C - 16:6 * C - 16].bitcast(BF16).rearrange("p (t j) -> p t j", j=2), tile("dc1", [P, T, 2], BF16)[:]]
        da_slots = [shared[:, 2 * C:4 * C].bitcast(BF16), tile("da_slots1", [P, 4 * C], BF16)[:]]
        dh_copy = [shared[:, 1:2 * C + 1].rearrange("p (t j) -> p t j", j=2), tile("dh_sb1", [P, HALF, 2], F32)[:]]

        def product_v(dst, saved, th, first=0):
            nc.vector.tensor_tensor(
                out=dst[:, HALF * th + first:HALF * (th + 1), :].rearrange("p (g i) j -> p g j i", i=4),
                in0=dh[0, th][:, :, first:].rearrange("p j (g i) -> p g j i", i=4),
                in1=saved[0, th][:, :, first:].rearrange("p j (g i) -> p g j i", i=4),
                op=MULT,
            )

        def product_g(th):
            nc.scalar.copy(out=dh_copy[th], in_=dh[1, th][:].rearrange("p j t -> p t j"))
            nc.gpsimd.tensor_tensor(out=dc[1][:, halves[th], :], in0=dh_copy[th], in1=a_sb[1, th][:].rearrange("p j t -> p t j"), op=MULT)

        def gather_plane(slots, i, e):
            nc.scalar.activation(out=slots.rearrange("p (s j) -> p s j", j=4)[:, :, 2 + i], in_=da_hi[:, i, :].indirect(slots_of(list_a, e * C, C)), func=COPY)

        for th in range(2):
            nc.vector.tensor_tensor(out=da_hi[:, :, halves[th]], in0=dh[1, th][:], in1=c_sb[1, th][:], op=MULT)
        for th in range(2):
            product_v(da_lo, c_sb, th)
        product_g(0)
        gather_plane(da_slots[0], 0, 0)
        product_g(1)
        gather_plane(da_slots[0], 1, 0)
        dh_first = tile("dh_first", [P, FIRST, 2], F32)
        nc.scalar.copy(out=dh_first[:], in_=dh[0, 0][:, :, :FIRST].rearrange("p j t -> p t j"))
        product_v(dc[0], a_sb, 1)
        for e in (1, 0):
            gather_pairs(da_slots[e], 0, da_lo, list_a, e * C, C)
        product_v(dc[0], a_sb, 0, FIRST)
        for i in range(2):
            gather_plane(da_slots[1], i, 1)

        dc_slots = [tile(f"dc_slots{e}", [P, 4 * C], BF16)[:] for e in range(E)]
        r_ps, q_ps = {}, {}

        def expert_a(e, tag, sc_tag=None):
            quantized = quantize(f"da_q{e}", da_slots[e], C, tag, sc_tag)
            for kh in range(2):
                r_ps[e, kh] = bank(f"r_ps{e}{kh}", [P, C])
                expert_product(r_ps[e, kh][:], wa, wa_sc, e, kh, quantized)

        def expert_b(e):
            quantized = quantize(f"dc_q{e}", dc_slots[e], C, "dc_codes")
            for kh in range(2):
                q_ps[e, kh] = bank(f"q_ps{e}{kh}", [P, C], f"dh{e}{kh}")
                expert_product(q_ps[e, kh][:], wb, wb_sc, e, kh, quantized)

        expert_a(0, "dh_sb1")
        nc.gpsimd.tensor_tensor(out=dc[0][:, :FIRST, :], in0=dh_first[:], in1=a_sb[0, 0][:, :, :FIRST].rearrange("p j t -> p t j"), op=MULT)
        for e in range(E):
            gather_pairs(dc_slots[e], 1, dc[1], list_b, e * C, C)
        gather_pairs(dc_slots[0], 0, dc[0], list_b, 0, C)
        expert_a(1, "dc1", "dh_first")
        expert_b(0)
        gather_pairs(dc_slots[1], 0, dc[0], list_b, C, C)

        r_tok = [tile(f"r_tok{kh}", [P, T], F32) for kh in range(2)]
        q_tok = [tile(f"q_tok{kh}", [P, T], F32) for kh in range(2)]
        scatter_s(r_tok[0], leave_psum_s("r_sb00", r_ps[0, 0]), list_a, 0)
        scatter_s(r_tok[1], leave_psum_s("r_sb01", r_ps[0, 1]), list_a, 0)
        scatter_s(r_tok[0], leave_psum_v("r_sb10", r_ps[1, 0], "dc_slots0"), list_a, C)

        q_sb00 = leave_psum_v("q_sb00", q_ps[0, 0])
        expert_b(1)
        q_sb01 = leave_psum_v("q_sb01", q_ps[0, 1])
        scatter_v(q_tok[0], q_sb00, list_b, 0)
        scatter_s(q_tok[1], q_sb01, list_b, 0)
        q_sb10 = leave_psum_v("q_sb10", q_ps[1, 0])
        q_sb11 = leave_psum_v("q_sb11", q_ps[1, 1])
        r_sb11 = leave_psum_v("r_sb11", r_ps[1, 1], "q_sb00")
        scatter_v(q_tok[0], q_sb10, list_b, C)
        total = [tile(f"total{kh}", [P, T], F32) for kh in range(2)]
        nc.gpsimd.tensor_tensor(out=total[0][:], in0=r_tok[0][:], in1=q_tok[0][:], op=ADD)
        nc.sync.dma_start(out=out[0:P, :], in_=total[0][:])
        scatter_s(q_tok[1], q_sb11, list_b, C)
        scatter_v(r_tok[1], r_sb11, list_a, C)
        for th in range(2):
            nc.vector.tensor_tensor(out=total[1][:, halves[th]], in0=r_tok[1][:, halves[th]], in1=q_tok[1][:, halves[th]], op=ADD)
            (nc.scalar if th == 0 else nc.sync).dma_start(out=out[P:2 * P, halves[th]], in_=total[1][:, halves[th]])
